import numpy as np
import ml_dtypes


def mxq(x, axis, fmt="e4m3"):
    dtype, down = {"e4m3": (ml_dtypes.float8_e4m3fn, 7), "e5m2": (ml_dtypes.float8_e5m2, 14)}[fmt]
    v = np.moveaxis(np.asarray(x, np.float32).astype(ml_dtypes.bfloat16).astype(np.float64), axis, -1)
    blocks = v.reshape(v.shape[:-1] + (-1, 32))
    amax = np.abs(blocks).max(-1, keepdims=True)
    byte = np.maximum(np.where(amax > 0, np.frexp(amax)[1] - 1 + 127, 0) - down, 1)
    scale = np.exp2(byte - 127.0)
    codes = (blocks / scale).astype(np.float32).astype(dtype).astype(np.float64)
    return np.moveaxis((codes * scale).reshape(v.shape), -1, axis)


WIDE = False


def mx_kscale(k):
    if not WIDE:
        return np.ones(k)
    levels = np.array([10, -10, 5, -5, 0])
    if k % 512:
        return np.exp2(np.random.permutation(np.resize(levels, k // 32))).repeat(32)
    a = np.empty((k // 512, 16))
    for p in range(k // 512):
        a[p, :8] = np.random.permutation(np.resize(levels, 8))
        for g in range(8):
            far = levels[np.abs(levels - a[p, g]) >= 10]
            a[p, g + 8] = far[np.random.randint(len(far))]
    return np.exp2(a.ravel()).repeat(32)


BF16 = ml_dtypes.bfloat16


def bf(x):
    return np.asarray(x, np.float32).astype(BF16)


def f64(x):
    return np.asarray(x).astype(np.float64)

def planes(Y):
    n, m = Y.shape
    b = f64(bf(Y)).reshape(n // 32, 32, m)
    amax = np.abs(b).max(1)
    byte = np.clip(np.where(amax > 0, np.frexp(amax)[1] - 1 + 127 - 7, 1), 1, 254)
    codes = (b * np.exp2(127.0 - byte)[:, None, :]).reshape(n, m).astype(np.float32).astype(ml_dtypes.float8_e4m3fn).view(np.uint8)
    words = codes.reshape(n // 512, 128, 4, m).transpose(0, 1, 3, 2)
    return np.ascontiguousarray(words), np.ascontiguousarray(byte.astype(np.uint8).reshape(n // 512, 16, m))


R, B, N, C, E = 2, 128, 8, 512, 512


def split_features(x, w, bias):
    y = mxq(x.reshape(R, B * N, C), 2, "e4m3") @ mxq(w, 1, "e4m3")
    z = y.reshape(R, B, N, E) + bias[:, None, None, :]
    return np.maximum(z, 0.0)


def softmax_over_splits(l):
    shifted = l - np.max(l, axis=0, keepdims=True)
    e = np.exp(shifted)
    return e / np.sum(e, axis=0, keepdims=True)


def setup_inputs():
    s, t = mx_kscale(C), mx_kscale(E)
    return {"x": bf(np.random.standard_normal((R, B, N, C)) * s),
            "w": bf(np.random.standard_normal((R, C, E)) / np.sqrt(C) / s[:, None]),
            "bias": bf(np.random.standard_normal((R, E)) * 0.3),
            "gs": bf(np.random.standard_normal(E) * t),
            "wa": bf(np.random.standard_normal((R, E, E)) * 1.5 / np.sqrt(E) / t[:, None]),
            "ba": bf(np.random.standard_normal((R, E)) * 0.5)}


def core(x, w, bias, gs, wa, ba):
    u = split_features(f64(x), f64(w), f64(bias))
    s = np.mean(np.sum(u, axis=0), axis=1)
    sg = s * f64(gs)[None, :]
    l = (mxq(sg, 1, "e4m3") @ mxq(f64(wa), 1, "e4m3")) + f64(ba)[:, None, :]
    a = softmax_over_splits(l)
    return np.sum(a[:, :, None, :] * u, axis=0)


def reference(x, w, bias, gs, wa, ba):
    R_out = core(x, w, bias, gs, wa, ba)
    words, scales = planes(np.moveaxis(R_out, 2, 0).reshape(512, -1))
    return R_out, words, scales

@@ -1,0 +1,441 @@
+from contextlib import ExitStack
+
+import concourse.mybir as mybir
+from concourse.masks import make_identity
+
+F32 = mybir.dt.float32
+BF16 = mybir.dt.bfloat16
+U32 = mybir.dt.uint32
+I32 = mybir.dt.int32
+U8 = mybir.dt.uint8
+FP8X4 = mybir.dt.float8_e4m3fn_x4
+ADD = mybir.AluOpType.add
+SUB = mybir.AluOpType.subtract
+MUL = mybir.AluOpType.mult
+MAX = mybir.AluOpType.max
+AF = mybir.ActivationFunctionType
+
+R, B, N, C, E = 2, 128, 8, 512, 512
+T = B * N
+FLOPS = 2 * R * T * C * E + 2 * R * B * E * E
+
+CH = 256
+CB = CH // N
+NCH = T // CH
+HB = 64
+HT = HB * N
+
+
+def tile_radixsplitattentionpointwise_x1_kernel(tc, x, w, bias, gs, wa, ba, out_0, out_1, out_2):
+    nc = tc.nc
+    with ExitStack() as ctx:
+        sb = ctx.enter_context(tc.tile_pool(name="sb", bufs=1))
+        pp = ctx.enter_context(tc.psum_pool(name="pp", bufs=1))
+        ctx.enter_context(tc.manual_schedule())
+
+        def big(name, shape, dtype):
+            return sb.tile(shape, dtype, name=name, align_bytes=64)
+
+        brow = big("brow", [128, 512], BF16)
+        nc.vector.memset(brow[:], 0.0)
+        warm = big("warm", [128, 1], F32)
+        nc.vector.memset(warm[:], 0.0)
+        warm2 = big("warm2", [128, 1], F32)
+        nc.scalar.activation(out=warm2[:], in_=warm[:], func=AF.Sigmoid)
+        nc.scalar.dma_start(out=brow[0:2, :], in_=bias)
+        nc.scalar.dma_start(out=brow[2:3, :], in_=gs.unsqueeze(0))
+        nc.scalar.dma_start(out=brow[3:5, :], in_=ba)
+
+        identf = big("identf", [128, 128], F32)
+        make_identity(nc, identf[:])
+        identb = big("identb", [128, 128], BF16)
+        nc.vector.tensor_copy(out=identb[:], in_=identf[:])
+        sgc = big("sgc", [128, B], U32)
+        sgs = big("sgs", [128, B], U8)
+        nc.gpsimd.memset(sgc[:], 0)
+        nc.gpsimd.memset(sgs[:], 0)
+
+        xs = {}
+        xg = {}
+        xc = {}
+        xsc = {}
+        for c in range(NCH):
+            for r in range(R):
+                k = "%d%d" % (r, c)
+                xs[r, c] = big("xs" + k, [128, 1024], BF16)
+                xg[r, c] = big("xg" + k, [128, 1024], BF16)
+                xc[r, c] = big("xc" + k, [128, CH], U32)
+                xsc[r, c] = big("xsc" + k, [128, CH], U8)
+        wr = {}
+        wg = {}
+        wc = {}
+        ws = {}
+        for nm in ("w1", "w0", "a1", "a0"):
+            wr[nm] = big("wr" + nm, [128, 4, 512], BF16)
+            wg[nm] = big("wg" + nm, [128, 2048], BF16)
+            wc[nm] = big("wc" + nm, [128, 512], U32)
+            ws[nm] = big("ws" + nm, [128, 512], U8)
+        wsrc = {"w0": w[0], "w1": w[1], "a0": wa[0], "a1": wa[1]}
+
+        def load_x(r, c):
+            nc.sync.dma_start(
+                out=xs[r, c][:],
+                in_=x[r, CB * c : CB * (c + 1)].rearrange("b n c -> (b n) c").rearrange("(q j) c -> q (j c)", j=2),
+            )
+
+        def load_w(nm):
+            nc.sync.dma_start(out=wr[nm][:], in_=wsrc[nm].rearrange("(p j) c -> p j c", j=4))
+
+        load_x(1, 0)
+        load_w("w1")
+        load_x(0, 0)
+        load_w("w0")
+        load_x(1, 1)
+        load_x(0, 1)
+        load_w("a1")
+        load_w("a0")
+        load_x(1, 2)
+        load_x(0, 2)
+        load_x(1, 3)
+        load_x(0, 3)
+
+        vec = big("vec", [128, 5, 4], F32)
+        nb0 = big("nb0", [128, 4], F32)
+        b08 = big("b08", [128, 4], F32)
+        bd = big("bd", [128, 4], F32)
+        gsb = big("gsb", [128, HB, 4], F32)
+
+        ct = pp.tile([128, 4, 128], BF16, name="ct", tag="sum", bufs=1)
+
+        def consts_pe():
+            for t in range(4):
+                nc.tensor.transpose(ct[:, t, :], brow[:, t::4], identb[:])
+
+        def consts():
+            nc.vector.tensor_copy(out=vec[:], in_=ct[:, :, 0:5].rearrange("p t r -> p r t"))
+            nc.vector.tensor_scalar(out=nb0[:], in0=vec[:, 0, :], scalar1=-1.0, scalar2=None, op0=MUL)
+            nc.vector.tensor_scalar(out=b08[:], in0=vec[:, 0, :], scalar1=8.0, scalar2=None, op0=MUL)
+            nc.vector.tensor_sub(out=bd[:], in0=vec[:, 3, :], in1=vec[:, 4, :])
+            nc.vector.tensor_scalar(
+                out=gsb[:], in0=vec[:, 2:3, :].to_broadcast([128, HB, 4]), scalar1=0.125, scalar2=None, op0=MUL
+            )
+
+        xt = {}
+
+        def x_tr(r, c):
+            ps = pp.tile([128, 2, 2, 128], F32, name="xt%d%d" % (r, c), tag="tp", bufs=2)
+            xt[r, c] = ps
+            words = xs[r, c][:].bitcast(F32)
+            for j in range(2):
+                for u in range(2):
+                    nc.tensor.transpose(ps[:, j, u, :], words[:, 256 * j + u : 256 * (j + 1) : 2], identf[:])
+
+        def x_cp(r, c, eng):
+            dst = xg[r, c][:].bitcast(F32).rearrange("p (q j u) -> p q j u", j=2, u=2)
+            src = xt[r, c][:].rearrange("p j u q -> p q j u")
+            if eng == "v":
+                nc.vector.tensor_copy(out=dst, in_=src)
+            else:
+                nc.scalar.copy(out=dst, in_=src)
+
+        def x_q(r, c):
+            nc.vector.quantize_mx(out=xc[r, c][:].bitcast(FP8X4), scales=xsc[r, c][:], in_=xg[r, c][:])
+
+        def w_cp(nm, t0, t1, eng):
+            dst = wg[nm][:].rearrange("p (t m j) -> p t m j", t=4, j=4)[:, t0:t1]
+            src = wr[nm][:].rearrange("p j (m t) -> p t m j", t=4)[:, t0:t1]
+            if eng == "v":
+                nc.vector.tensor_copy(out=dst, in_=src)
+            elif eng == "s":
+                nc.scalar.copy(out=dst, in_=src)
+            else:
+                sign = -1.0 if nm == "a1" else 1.0
+                nc.gpsimd.tensor_scalar(out=dst, in0=src, scalar1=sign, scalar2=0.0, op0=MUL, op1=ADD)
+
+        def w_q(nm, t0, t1):
+            nc.vector.quantize_mx(
+                out=wc[nm][:, 128 * t0 : 128 * t1].bitcast(FP8X4),
+                scales=ws[nm][:, 128 * t0 : 128 * t1],
+                in_=wg[nm][:, 512 * t0 : 512 * t1],
+            )
+
+        z = {}
+        u1 = {}
+        sg = {}
+        dd = {}
+        mm = {}
+        ob = {}
+        oc = {}
+        osc = {}
+        for h in range(2):
+            k = "%d" % h
+            u1[h] = big("u1" + k, [128, 4, HT], F32)
+            sg[h] = big("sg" + k, [128, 4, HT], F32)
+            dd[h] = big("dd" + k, [128, 4, HT], F32)
+            mm[h] = big("mm" + k, [128, 4, HT], F32)
+            ob[h] = big("ob" + k, [128, HT, 4], BF16)
+            oc[h] = big("oc" + k, [128, HT], U32)
+            osc[h] = big("osc" + k, [128, HT], U8)
+
+        def mx1(r, c):
+            for i in range(2):
+                ps = pp.tile([128, 2, CH], F32, name="z%d%d%d" % (r, c, i), tag="z%d" % r, bufs=2)
+                z[r, c, i] = ps
+                for k in range(2):
+                    t = 2 * i + k
+                    nc.tensor.matmul_mx(
+                        out=ps[:, k, :],
+                        lhsT=wc["w%d" % r][:, 128 * t : 128 * (t + 1)].bitcast(FP8X4),
+                        lhsT_scale=ws["w%d" % r][:, 128 * t : 128 * (t + 1)],
+                        rhs=xc[r, c][:].bitcast(FP8X4),
+                        rhs_scale=xsc[r, c][:],
+                        start=True,
+                        stop=True,
+                    )
+
+        def cols(c):
+            h, o = divmod(c, 2)
+            return h, slice(CH * o, CH * (o + 1))
+
+        def relu(c):
+            h, s = cols(c)
+            for t in range(4):
+                nc.scalar.activation(
+                    out=u1[h][:, t, s], in_=z[1, c, t // 2][:, t % 2, :], func=AF.Relu, bias=vec[:, 1, t : t + 1]
+                )
+
+        def sigma(c):
+            h, s = cols(c)
+            for t in range(4):
+                nc.vector.scalar_tensor_tensor(
+                    out=sg[h][:, t, s], in0=z[0, c, t // 2][:, t % 2, :], scalar=nb0[:, t : t + 1],
+                    in1=u1[h][:, t, s], op0=MAX, op1=ADD,
+                )
+
+        def diff(c):
+            h, s = cols(c)
+            for t in range(4):
+                nc.vector.scalar_tensor_tensor(
+                    out=dd[h][:, t, s], in0=z[0, c, t // 2][:, t % 2, :], scalar=nb0[:, t : t + 1],
+                    in1=u1[h][:, t, s], op0=MAX, op1=SUB,
+                )
+
+        pss = {}
+
+        def psum_sum(c):
+            h, s = cols(c)
+            o = c % 2
+            if o == 0:
+                pss[h] = pp.tile([128, 2, 4, CB], F32, name="pss%d" % h, tag="sum", bufs=1)
+            for n in range(7):
+                nc.tensor.matmul(
+                    out=pss[h][:, o, :, :],
+                    lhsT=identf[:],
+                    rhs=sg[h][:, :, CH * o + n : CH * (o + 1) : N],
+                    start=(n == 0),
+                    stop=(n == 6),
+                )
+
+        s2 = {}
+        sgb = {}
+        for h in range(2):
+            s2[h] = big("s2%d" % h, [128, 4, HB], F32)
+            sgb[h] = big("sgb%d" % h, [128, HB, 4], BF16)
+
+        def squeeze_s(h):
+            for t in range(4):
+                nc.vector.scalar_tensor_tensor(
+                    out=s2[h][:, t, :].rearrange("p (o b) -> p o b", o=2),
+                    in0=sg[h][:, t, 7::N].rearrange("p (o b) -> p o b", o=2),
+                    scalar=b08[:, t : t + 1],
+                    in1=pss[h][:, :, t, :],
+                    op0=ADD,
+                    op1=ADD,
+                )
+
+        def sgate(h):
+            nc.vector.tensor_mul(out=sgb[h][:], in0=s2[h][:].rearrange("p t b -> p b t"), in1=gsb[:])
+
+        def sg_q(h):
+            nc.vector.quantize_mx(
+                out=sgc[:, HB * h : HB * (h + 1)].bitcast(FP8X4),
+                scales=sgs[:, HB * h : HB * (h + 1)],
+                in_=sgb[h][:].rearrange("p b t -> p (b t)"),
+            )
+
+        lps = {}
+        a0 = {}
+        for h in range(2):
+            a0[h] = big("a0g%d" % h, [128, 4, HB], F32)
+
+        def mx2(h):
+            lps[h] = pp.tile([128, 4, B], F32, name="l%d" % h, tag="l", bufs=1)
+            for t in range(4):
+                for i, nm in enumerate(("a0", "a1")):
+                    nc.tensor.matmul_mx(
+                        out=lps[h][:, t, :],
+                        lhsT=wc[nm][:, 128 * t : 128 * (t + 1)].bitcast(FP8X4),
+                        lhsT_scale=ws[nm][:, 128 * t : 128 * (t + 1)],
+                        rhs=sgc[:].bitcast(FP8X4),
+                        rhs_scale=sgs[:],
+                        start=(i == 0),
+                        stop=(i == 1),
+                    )
+
+        def sigm(h):
+            for t in range(4):
+                nc.scalar.activation(
+                    out=a0[h][:, t, :], in_=lps[h][:, t, HB * h : HB * (h + 1)], func=AF.Sigmoid, bias=bd[:, t : t + 1]
+                )
+
+        def mul_a(h):
+            for t in range(4):
+                nc.vector.scalar_tensor_tensor(
+                    out=mm[h][:, t, :].rearrange("p (b n) -> p b n", n=N),
+                    in0=dd[h][:, t, :].rearrange("p (b n) -> p b n", n=N),
+                    scalar=vec[:, 0, t : t + 1],
+                    in1=a0[h][:, t, :].unsqueeze(2).to_broadcast([128, HB, N]),
+                    op0=ADD,
+                    op1=MUL,
+                )
+
+        def obf(h, j):
+            s = slice(128 * j, 128 * (j + 1))
+            nc.vector.tensor_add(
+                out=ob[h][:, s, :],
+                in0=mm[h][:, :, s].rearrange("p t k -> p k t"),
+                in1=u1[h][:, :, s].rearrange("p t k -> p k t"),
+            )
+
+        def o_q(h, j0, j1):
+            s = slice(128 * j0, 128 * j1)
+            nc.vector.quantize_mx(
+                out=oc[h][:, s].bitcast(FP8X4), scales=osc[h][:, s], in_=ob[h][:, s, :].rearrange("p k t -> p (k t)")
+            )
+
+        ops = {}
+        ot = {}
+
+        def o_tr(h, j):
+            s = slice(128 * j, 128 * (j + 1))
+            ps = pp.tile([128, 4, 128], F32, name="o%d%d" % (h, j), tag="tp" if j % 2 == 0 else "z1", bufs=2)
+            ops[h, j] = ps
+            for t in range(4):
+                nc.tensor.matmul(out=ps[:, t, :], lhsT=u1[h][:, t, s], rhs=identf[:], start=True, stop=False, is_transpose=True)
+                nc.tensor.matmul(out=ps[:, t, :], lhsT=mm[h][:, t, s], rhs=identf[:], start=False, stop=True, is_transpose=True)
+
+        def o_cp(h, j, eng):
+            ot[h, j] = big("ot%d%d" % (h, j), [128, 128, 4], F32)
+            src = ops[h, j][:].rearrange("q t p -> q p t")
+            if eng == "v":
+                nc.vector.tensor_copy(out=ot[h, j][:], in_=src)
+            else:
+                nc.scalar.copy(out=ot[h, j][:], in_=src)
+
+        rows = out_0.rearrange("b n e -> (b n) e")
+        words = out_1.rearrange("g p m t -> (g p) (m t)").bitcast(I32)
+        srows = out_2.rearrange("g q m -> (g q) m").bitcast(I32)
+
+        def o_st(h, j):
+            r0 = HT * h + 128 * j
+            nc.sync.dma_start(out=rows[r0 : r0 + 128, :], in_=ot[h, j][:].rearrange("q p t -> q (p t)"))
+
+        def w_st(h):
+            nc.sync.dma_start(out=words[:, HT * h : HT * (h + 1)], in_=oc[h][:].bitcast(I32))
+            for q in range(4):
+                nc.scalar.dma_start(
+                    out=srows[4 * q : 4 * q + 4, HT // 4 * h : HT // 4 * (h + 1)],
+                    in_=osc[h][32 * q : 32 * q + 4, :].bitcast(I32),
+                )
+
+        x_tr(1, 0)
+        x_cp(1, 0, "s")
+        x_tr(0, 0)
+        consts_pe()
+        w_cp("w1", 0, 2, "v")
+        w_cp("w1", 2, 4, "s")
+        x_q(1, 0)
+        w_q("w1", 0, 2)
+        x_cp(0, 0, "v")
+        w_q("w1", 2, 4)
+        mx1(1, 0)
+        consts()
+        x_q(0, 0)
+        w_cp("w0", 0, 2, "v")
+        w_cp("w0", 2, 4, "s")
+        x_tr(1, 1)
+        relu(0)
+        w_q("w0", 0, 2)
+        x_cp(1, 1, "v")
+        w_q("w0", 2, 4)
+        mx1(0, 0)
+        x_tr(0, 1)
+        x_q(1, 1)
+        mx1(1, 1)
+        sigma(0)
+        x_cp(0, 1, "s")
+        x_q(0, 1)
+        mx1(0, 1)
+        relu(1)
+        diff(0)
+        psum_sum(0)
+        w_cp("a1", 0, 4, "g")
+        w_cp("a0", 0, 4, "g")
+        x_tr(1, 2)
+        x_tr(0, 2)
+        sigma(1)
+        x_cp(1, 2, "s")
+        x_cp(0, 2, "s")
+        psum_sum(1)
+        x_q(1, 2)
+        diff(1)
+        x_q(0, 2)
+        mx1(1, 2)
+        mx1(0, 2)
+        relu(2)
+        w_q("a1", 0, 4)
+        w_q("a0", 0, 4)
+        squeeze_s(0)
+        x_tr(1, 3)
+        x_tr(0, 3)
+        sgate(0)
+        sg_q(0)
+        mx2(0)
+        x_cp(1, 3, "s")
+        x_cp(0, 3, "s")
+        sigma(2)
+        sigm(0)
+        x_q(1, 3)
+        x_q(0, 3)
+        mx1(1, 3)
+        mx1(0, 3)
+        psum_sum(2)
+        diff(2)
+        relu(3)
+        sigma(3)
+        psum_sum(3)
+        diff(3)
+        mul_a(0)
+        for j in range(4):
+            o_tr(0, j)
+            o_cp(0, j, "s")
+            o_st(0, j)
+        squeeze_s(1)
+        obf(0, 0)
+        sgate(1)
+        obf(0, 1)
+        sg_q(1)
+        mx2(1)
+        sigm(1)
+        obf(0, 2)
+        obf(0, 3)
+        mul_a(1)
+        o_q(0, 0, 4)
+        w_st(0)
+        for j in range(4):
+            o_tr(1, j)
+            obf(1, j)
+            o_cp(1, j, "s")
+            o_st(1, j)
+        o_q(1, 0, 4)
+        w_st(1)

@@ -10,7 +10,6 @@ I32 = mybir.dt.int32
 U8 = mybir.dt.uint8
 FP8X4 = mybir.dt.float8_e4m3fn_x4
 ADD = mybir.AluOpType.add
-SUB = mybir.AluOpType.subtract
 MUL = mybir.AluOpType.mult
 MAX = mybir.AluOpType.max
 AF = mybir.ActivationFunctionType
@@ -48,8 +47,15 @@ def tile_radixsplitattentionpointwise_x1_kernel(tc, x, w, bias, gs, wa, ba, out_
 
         identf = big("identf", [128, 128], F32)
         make_identity(nc, identf[:])
+        perm = big("perm", [128, 128], F32)
+        nc.vector.tensor_copy(
+            out=perm[:].rearrange("p (k b h) -> p k b h", k=2, h=2),
+            in_=identf[:].rearrange("p (b k h) -> p k b h", k=2, h=2),
+        )
         identb = big("identb", [128, 128], BF16)
         nc.vector.tensor_copy(out=identb[:], in_=identf[:])
+        grp = big("grp", [128, CB], F32)
+        nc.vector.reduce_sum(out=grp[:], in_=identf[:].rearrange("p (b n) -> p b n", n=4), axis=mybir.AxisListType.X)
         sgc = big("sgc", [128, B], U32)
         sgs = big("sgs", [128, B], U8)
         nc.gpsimd.memset(sgc[:], 0)
@@ -100,12 +106,9 @@ def tile_radixsplitattentionpointwise_x1_kernel(tc, x, w, bias, gs, wa, ba, out_
         load_x(0, 3)
 
         vec = big("vec", [128, 5, 4], F32)
-        nb0 = big("nb0", [128, 4], F32)
-        b08 = big("b08", [128, 4], F32)
         bd = big("bd", [128, 4], F32)
-        gsb = big("gsb", [128, HB, 4], F32)
-
-        ct = pp.tile([128, 4, 128], BF16, name="ct", tag="sum", bufs=1)
+        gsb = big("gsb", [128, CB, 4], F32)
+        ct = pp.tile([128, 4, 128], BF16, name="ct", tag="st", bufs=2)
 
         def consts_pe():
             for t in range(4):
@@ -113,11 +116,11 @@ def tile_radixsplitattentionpointwise_x1_kernel(tc, x, w, bias, gs, wa, ba, out_
 
         def consts():
             nc.vector.tensor_copy(out=vec[:], in_=ct[:, :, 0:5].rearrange("p t r -> p r t"))
-            nc.vector.tensor_scalar(out=nb0[:], in0=vec[:, 0, :], scalar1=-1.0, scalar2=None, op0=MUL)
-            nc.vector.tensor_scalar(out=b08[:], in0=vec[:, 0, :], scalar1=8.0, scalar2=None, op0=MUL)
+
+        def consts2():
             nc.vector.tensor_sub(out=bd[:], in0=vec[:, 3, :], in1=vec[:, 4, :])
             nc.vector.tensor_scalar(
-                out=gsb[:], in0=vec[:, 2:3, :].to_broadcast([128, HB, 4]), scalar1=0.125, scalar2=None, op0=MUL
+                out=gsb[:], in0=vec[:, 2:3, :].to_broadcast([128, CB, 4]), scalar1=0.125, scalar2=None, op0=MUL
             )
 
         xt = {}
@@ -128,7 +131,7 @@ def tile_radixsplitattentionpointwise_x1_kernel(tc, x, w, bias, gs, wa, ba, out_
             words = xs[r, c][:].bitcast(F32)
             for j in range(2):
                 for u in range(2):
-                    nc.tensor.transpose(ps[:, j, u, :], words[:, 256 * j + u : 256 * (j + 1) : 2], identf[:])
+                    nc.tensor.transpose(ps[:, j, u, :], words[:, 256 * j + u : 256 * (j + 1) : 2], perm[:])
 
         def x_cp(r, c, eng):
             dst = xg[r, c][:].bitcast(F32).rearrange("p (q j u) -> p q j u", j=2, u=2)
@@ -145,12 +148,14 @@ def tile_radixsplitattentionpointwise_x1_kernel(tc, x, w, bias, gs, wa, ba, out_
             dst = wg[nm][:].rearrange("p (t m j) -> p t m j", t=4, j=4)[:, t0:t1]
             src = wr[nm][:].rearrange("p j (m t) -> p t m j", t=4)[:, t0:t1]
             if eng == "v":
-                nc.vector.tensor_copy(out=dst, in_=src)
-            elif eng == "s":
-                nc.scalar.copy(out=dst, in_=src)
+                if nm == "a1":
+                    nc.vector.tensor_scalar(out=dst, in0=src, scalar1=-1.0, scalar2=None, op0=MUL)
+                else:
+                    nc.vector.tensor_copy(out=dst, in_=src)
+            elif nm == "a1":
+                nc.scalar.activation(out=dst, in_=src, func=AF.Copy, scale=-1.0)
             else:
-                sign = -1.0 if nm == "a1" else 1.0
-                nc.gpsimd.tensor_scalar(out=dst, in0=src, scalar1=sign, scalar2=0.0, op0=MUL, op1=ADD)
+                nc.scalar.copy(out=dst, in_=src)
 
         def w_q(nm, t0, t1):
             nc.vector.quantize_mx(
@@ -160,8 +165,7 @@ def tile_radixsplitattentionpointwise_x1_kernel(tc, x, w, bias, gs, wa, ba, out_
             )
 
         z = {}
-        u1 = {}
-        sg = {}
+        u = {}
         dd = {}
         mm = {}
         ob = {}
@@ -169,8 +173,8 @@ def tile_radixsplitattentionpointwise_x1_kernel(tc, x, w, bias, gs, wa, ba, out_
         osc = {}
         for h in range(2):
             k = "%d" % h
-            u1[h] = big("u1" + k, [128, 4, HT], F32)
-            sg[h] = big("sg" + k, [128, 4, HT], F32)
+            u[0, h] = big("u0" + k, [128, 4, HT], F32)
+            u[1, h] = big("u1" + k, [128, 4, HT], F32)
             dd[h] = big("dd" + k, [128, 4, HT], F32)
             mm[h] = big("mm" + k, [128, 4, HT], F32)
             ob[h] = big("ob" + k, [128, HT, 4], BF16)
@@ -179,7 +183,7 @@ def tile_radixsplitattentionpointwise_x1_kernel(tc, x, w, bias, gs, wa, ba, out_
 
         def mx1(r, c):
             for i in range(2):
-                ps = pp.tile([128, 2, CH], F32, name="z%d%d%d" % (r, c, i), tag="z%d" % r, bufs=2)
+                ps = pp.tile([128, 2, CH], F32, name="z%d%d%d" % (r, c, i), tag="z", bufs=3)
                 z[r, c, i] = ps
                 for k in range(2):
                     t = 2 * i + k
@@ -197,64 +201,60 @@ def tile_radixsplitattentionpointwise_x1_kernel(tc, x, w, bias, gs, wa, ba, out_
             h, o = divmod(c, 2)
             return h, slice(CH * o, CH * (o + 1))
 
-        def relu(c):
+        def relu(r, c, eng="ssss"):
             h, s = cols(c)
             for t in range(4):
-                nc.scalar.activation(
-                    out=u1[h][:, t, s], in_=z[1, c, t // 2][:, t % 2, :], func=AF.Relu, bias=vec[:, 1, t : t + 1]
-                )
-
-        def sigma(c):
-            h, s = cols(c)
-            for t in range(4):
-                nc.vector.scalar_tensor_tensor(
-                    out=sg[h][:, t, s], in0=z[0, c, t // 2][:, t % 2, :], scalar=nb0[:, t : t + 1],
-                    in1=u1[h][:, t, s], op0=MAX, op1=ADD,
-                )
+                if eng[t] == "s":
+                    nc.scalar.activation(
+                        out=u[r, h][:, t, s], in_=z[r, c, t // 2][:, t % 2, :], func=AF.Relu, bias=vec[:, r, t : t + 1]
+                    )
+                else:
+                    nc.vector.tensor_scalar(
+                        out=u[r, h][:, t, s], in0=z[r, c, t // 2][:, t % 2, :], scalar1=vec[:, r, t : t + 1],
+                        scalar2=0.0, op0=ADD, op1=MAX,
+                    )
 
         def diff(c):
             h, s = cols(c)
-            for t in range(4):
-                nc.vector.scalar_tensor_tensor(
-                    out=dd[h][:, t, s], in0=z[0, c, t // 2][:, t % 2, :], scalar=nb0[:, t : t + 1],
-                    in1=u1[h][:, t, s], op0=MAX, op1=SUB,
-                )
+            nc.vector.tensor_sub(out=dd[h][:, :, s], in0=u[0, h][:, :, s], in1=u[1, h][:, :, s])
 
+        pst = {}
+        ut = {}
         pss = {}
 
-        def psum_sum(c):
-            h, s = cols(c)
-            o = c % 2
-            if o == 0:
-                pss[h] = pp.tile([128, 2, 4, CB], F32, name="pss%d" % h, tag="sum", bufs=1)
-            for n in range(7):
-                nc.tensor.matmul(
-                    out=pss[h][:, o, :, :],
-                    lhsT=identf[:],
-                    rhs=sg[h][:, :, CH * o + n : CH * (o + 1) : N],
-                    start=(n == 0),
-                    stop=(n == 6),
-                )
+        def sum_t(c):
+            h, o = divmod(c, 2)
+            pst[c] = pp.tile([128, 4, 128], F32, name="pst%d" % c, tag="st", bufs=2)
+            for t in range(4):
+                for i in range(4):
+                    r, k2 = 1 - i // 2, i % 2
+                    s = CH * o + 128 * k2
+                    nc.tensor.matmul(
+                        out=pst[c][:, t, :], lhsT=u[r, h][:, t, s : s + 128], rhs=identf[:],
+                        start=(i == 0), stop=(i == 3), is_transpose=True,
+                    )
 
-        s2 = {}
+        def sum_cp(c, eng):
+            ut[c] = big("ut%d" % c, [128, 4, 128], F32)
+            if eng == "v":
+                nc.vector.tensor_copy(out=ut[c][:], in_=pst[c][:])
+            else:
+                nc.scalar.copy(out=ut[c][:], in_=pst[c][:])
+
+        def sum_g(c):
+            pss[c] = pp.tile([128, 4, CB], F32, name="pss%d" % c, tag="st", bufs=2)
+            for t in range(4):
+                nc.tensor.matmul(out=pss[c][:, t, :], lhsT=ut[c][:, t, :], rhs=grp[:], start=True, stop=True)
+
         sgb = {}
         for h in range(2):
-            s2[h] = big("s2%d" % h, [128, 4, HB], F32)
             sgb[h] = big("sgb%d" % h, [128, HB, 4], BF16)
 
-        def squeeze_s(h):
-            for t in range(4):
-                nc.vector.scalar_tensor_tensor(
-                    out=s2[h][:, t, :].rearrange("p (o b) -> p o b", o=2),
-                    in0=sg[h][:, t, 7::N].rearrange("p (o b) -> p o b", o=2),
-                    scalar=b08[:, t : t + 1],
-                    in1=pss[h][:, :, t, :],
-                    op0=ADD,
-                    op1=ADD,
-                )
-
-        def sgate(h):
-            nc.vector.tensor_mul(out=sgb[h][:], in0=s2[h][:].rearrange("p t b -> p b t"), in1=gsb[:])
+        def sgate(c):
+            h, o = divmod(c, 2)
+            nc.vector.tensor_mul(
+                out=sgb[h][:, CB * o : CB * (o + 1), :], in0=pss[c][:].rearrange("p t b -> p b t"), in1=gsb[:]
+            )
 
         def sg_q(h):
             nc.vector.quantize_mx(
@@ -288,27 +288,29 @@ def tile_radixsplitattentionpointwise_x1_kernel(tc, x, w, bias, gs, wa, ba, out_
                     out=a0[h][:, t, :], in_=lps[h][:, t, HB * h : HB * (h + 1)], func=AF.Sigmoid, bias=bd[:, t : t + 1]
                 )
 
-        def mul_a(h):
-            for t in range(4):
-                nc.vector.scalar_tensor_tensor(
-                    out=mm[h][:, t, :].rearrange("p (b n) -> p b n", n=N),
-                    in0=dd[h][:, t, :].rearrange("p (b n) -> p b n", n=N),
-                    scalar=vec[:, 0, t : t + 1],
-                    in1=a0[h][:, t, :].unsqueeze(2).to_broadcast([128, HB, N]),
-                    op0=ADD,
-                    op1=MUL,
-                )
+        def blk(c, k2):
+            h, o = divmod(c, 2)
+            s = CH * o + 128 * k2
+            return h, o, slice(s, s + 128)
 
-        def obf(h, j):
-            s = slice(128 * j, 128 * (j + 1))
-            nc.vector.tensor_add(
-                out=ob[h][:, s, :],
-                in0=mm[h][:, :, s].rearrange("p t k -> p k t"),
-                in1=u1[h][:, :, s].rearrange("p t k -> p k t"),
+        def mul_a(c, k2):
+            h, o, s = blk(c, k2)
+            nc.vector.tensor_mul(
+                out=mm[h][:, :, s].rearrange("p t (b n) -> p t b n", n=4),
+                in0=dd[h][:, :, s].rearrange("p t (b n) -> p t b n", n=4),
+                in1=a0[h][:, :, CB * o : CB * (o + 1)].unsqueeze(3).to_broadcast([128, 4, CB, 4]),
             )
 
-        def o_q(h, j0, j1):
-            s = slice(128 * j0, 128 * j1)
+        def obf(c, k2):
+            h, o, s = blk(c, k2)
+            nc.vector.tensor_add(
+                out=ob[h][:].rearrange("p (o b k n) t -> p o k b t n", o=2, k=2, n=4)[:, o, k2],
+                in0=mm[h][:, :, s].rearrange("p t (b n) -> p b t n", n=4),
+                in1=u[1, h][:, :, s].rearrange("p t (b n) -> p b t n", n=4),
+            )
+
+        def o_q(h, c0, c1):
+            s = slice(CH * c0, CH * c1)
             nc.vector.quantize_mx(
                 out=oc[h][:, s].bitcast(FP8X4), scales=osc[h][:, s], in_=ob[h][:, s, :].rearrange("p k t -> p (k t)")
             )
@@ -316,126 +318,166 @@ def tile_radixsplitattentionpointwise_x1_kernel(tc, x, w, bias, gs, wa, ba, out_
         ops = {}
         ot = {}
 
-        def o_tr(h, j):
-            s = slice(128 * j, 128 * (j + 1))
-            ps = pp.tile([128, 4, 128], F32, name="o%d%d" % (h, j), tag="tp" if j % 2 == 0 else "z1", bufs=2)
-            ops[h, j] = ps
+        def o_tr(c, k2, tag="tp"):
+            h, o, s = blk(c, k2)
+            ps = pp.tile([128, 4, 128], F32, name="o%d%d" % (c, k2), tag=tag, bufs=3 if tag == "z" else 2)
+            ops[c, k2] = ps
             for t in range(4):
-                nc.tensor.matmul(out=ps[:, t, :], lhsT=u1[h][:, t, s], rhs=identf[:], start=True, stop=False, is_transpose=True)
+                nc.tensor.matmul(out=ps[:, t, :], lhsT=u[1, h][:, t, s], rhs=identf[:], start=True, stop=False, is_transpose=True)
                 nc.tensor.matmul(out=ps[:, t, :], lhsT=mm[h][:, t, s], rhs=identf[:], start=False, stop=True, is_transpose=True)
 
-        def o_cp(h, j, eng):
-            ot[h, j] = big("ot%d%d" % (h, j), [128, 128, 4], F32)
-            src = ops[h, j][:].rearrange("q t p -> q p t")
-            if eng == "v":
-                nc.vector.tensor_copy(out=ot[h, j][:], in_=src)
-            else:
-                nc.scalar.copy(out=ot[h, j][:], in_=src)
+        for c in range(NCH):
+            ot[c] = big("ot%d" % c, [128, 2, 128, 4], F32)
 
-        rows = out_0.rearrange("b n e -> (b n) e")
+        def o_cp(c, k2, eng):
+            src = ops[c, k2][:].rearrange("q t p -> q p t")
+            if eng == "v":
+                nc.vector.tensor_copy(out=ot[c][:, k2], in_=src)
+            else:
+                nc.scalar.copy(out=ot[c][:, k2], in_=src)
+
         words = out_1.rearrange("g p m t -> (g p) (m t)").bitcast(I32)
         srows = out_2.rearrange("g q m -> (g q) m").bitcast(I32)
 
-        def o_st(h, j):
-            r0 = HT * h + 128 * j
-            nc.sync.dma_start(out=rows[r0 : r0 + 128, :], in_=ot[h, j][:].rearrange("q p t -> q (p t)"))
+        def o_st(c):
+            for n in range(4):
+                nc.sync.dma_start(
+                    out=out_0[CB * c : CB * (c + 1), n::4, :], in_=ot[c][n::4].rearrange("q k p t -> q k (p t)")
+                )
+
+        def o_st1(c, k2):
+            for n in range(4):
+                nc.sync.dma_start(
+                    out=out_0[CB * c : CB * (c + 1), 4 * k2 + n, :], in_=ot[c][n::4, k2].rearrange("q p t -> q (p t)")
+                )
 
         def w_st(h):
             nc.sync.dma_start(out=words[:, HT * h : HT * (h + 1)], in_=oc[h][:].bitcast(I32))
             for q in range(4):
-                nc.scalar.dma_start(
+                nc.sync.dma_start(
                     out=srows[4 * q : 4 * q + 4, HT // 4 * h : HT // 4 * (h + 1)],
                     in_=osc[h][32 * q : 32 * q + 4, :].bitcast(I32),
                 )
 
-        x_tr(1, 0)
-        x_cp(1, 0, "s")
-        x_tr(0, 0)
-        consts_pe()
-        w_cp("w1", 0, 2, "v")
         w_cp("w1", 2, 4, "s")
+        x_tr(1, 0)
+        x_cp(1, 0, "v")
+        w_cp("w1", 0, 2, "v")
         x_q(1, 0)
+        consts_pe()
+        consts()
+        x_tr(0, 0)
         w_q("w1", 0, 2)
-        x_cp(0, 0, "v")
         w_q("w1", 2, 4)
         mx1(1, 0)
-        consts()
-        x_q(0, 0)
+        x_cp(0, 0, "s")
         w_cp("w0", 0, 2, "v")
-        w_cp("w0", 2, 4, "s")
-        x_tr(1, 1)
-        relu(0)
         w_q("w0", 0, 2)
+        x_q(0, 0)
+        x_tr(1, 1)
         x_cp(1, 1, "v")
+        w_cp("w0", 2, 4, "s")
+        x_tr(0, 1)
+        relu(1, 0, "ssss")
         w_q("w0", 2, 4)
         mx1(0, 0)
-        x_tr(0, 1)
+        relu(0, 0, "ssss")
         x_q(1, 1)
         mx1(1, 1)
-        sigma(0)
-        x_cp(0, 1, "s")
+        relu(1, 1, "ssss")
+        sum_t(0)
+        x_tr(1, 2)
+        x_cp(0, 1, "v")
         x_q(0, 1)
         mx1(0, 1)
-        relu(1)
-        diff(0)
-        psum_sum(0)
-        w_cp("a1", 0, 4, "g")
-        w_cp("a0", 0, 4, "g")
-        x_tr(1, 2)
+        w_cp("a1", 0, 4, "s")
+        w_cp("a0", 0, 4, "v")
+        relu(0, 1, "vvvv")
         x_tr(0, 2)
-        sigma(1)
+        sum_cp(0, "s")
+        sum_t(1)
         x_cp(1, 2, "s")
-        x_cp(0, 2, "s")
-        psum_sum(1)
-        x_q(1, 2)
-        diff(1)
-        x_q(0, 2)
-        mx1(1, 2)
-        mx1(0, 2)
-        relu(2)
         w_q("a1", 0, 4)
-        w_q("a0", 0, 4)
-        squeeze_s(0)
+        sum_cp(1, "s")
         x_tr(1, 3)
-        x_tr(0, 3)
-        sgate(0)
-        sg_q(0)
-        mx2(0)
+        consts2()
+        w_q("a0", 0, 4)
+        x_cp(0, 2, "v")
         x_cp(1, 3, "s")
-        x_cp(0, 3, "s")
-        sigma(2)
-        sigm(0)
+        x_q(1, 2)
+        x_q(0, 2)
+        sum_g(0)
+        sgate(0)
+        sum_g(1)
         x_q(1, 3)
-        x_q(0, 3)
-        mx1(1, 3)
-        mx1(0, 3)
-        psum_sum(2)
-        diff(2)
-        relu(3)
-        sigma(3)
-        psum_sum(3)
-        diff(3)
-        mul_a(0)
-        for j in range(4):
-            o_tr(0, j)
-            o_cp(0, j, "s")
-            o_st(0, j)
-        squeeze_s(1)
-        obf(0, 0)
         sgate(1)
+        sg_q(0)
+        mx1(1, 2)
+        mx2(0)
+        diff(1)
+        relu(1, 2, "ssss")
+        diff(0)
+        mx1(0, 2)
+        x_tr(0, 3)
+        sigm(0)
+        mul_a(1, 1)
+        mul_a(0, 1)
+        relu(0, 2, "ssss")
+        mul_a(0, 0)
+        sum_t(2)
+        x_cp(0, 3, "s")
+        x_q(0, 3)
+        mul_a(1, 0)
+        diff(2)
+        obf(0, 0)
+        sum_cp(2, "s")
+        obf(1, 0)
+        mx1(1, 3)
+        relu(1, 3, "ssss")
+        o_tr(0, 1)
+        mx1(0, 3)
+        relu(0, 3, "ssss")
+        sum_t(3)
+        diff(3)
+        o_tr(1, 1)
         obf(0, 1)
+        sum_cp(3, "s")
+        sum_g(2)
+        o_cp(1, 1, "s")
+        o_cp(0, 1, "s")
+        sgate(2)
+        sum_g(3)
+        sgate(3)
         sg_q(1)
         mx2(1)
+        o_tr(1, 0)
         sigm(1)
-        obf(0, 2)
-        obf(0, 3)
-        mul_a(1)
-        o_q(0, 0, 4)
+        o_cp(1, 0, "s")
+        o_tr(0, 0)
+        obf(1, 1)
+        o_q(0, 0, 2)
         w_st(0)
-        for j in range(4):
-            o_tr(1, j)
-            obf(1, j)
-            o_cp(1, j, "s")
-            o_st(1, j)
-        o_q(1, 0, 4)
+        o_cp(0, 0, "s")
+        mul_a(2, 0)
+        o_st(1)
+        o_tr(2, 0)
+        o_st(0)
+        mul_a(3, 0)
+        o_cp(2, 0, "s")
+        mul_a(2, 1)
+        o_tr(3, 0, "z")
+        o_cp(3, 0, "s")
+        mul_a(3, 1)
+        o_tr(3, 1)
+        o_tr(2, 1, "z")
+        o_cp(3, 1, "s")
+        o_st1(3, 1)
+        o_st1(3, 0)
+        obf(3, 0)
+        o_cp(2, 1, "s")
+        obf(3, 1)
+        obf(2, 1)
+        obf(2, 0)
+        o_q(1, 0, 2)
+        o_st(2)
         w_st(1)

@@ -56,10 +56,14 @@ def tile_radixsplitattentionpointwise_x1_kernel(tc, x, w, bias, gs, wa, ba, out_
         nc.vector.tensor_copy(out=identb[:], in_=identf[:])
         grp = big("grp", [128, CB], F32)
         nc.vector.reduce_sum(out=grp[:], in_=identf[:].rearrange("p (b n) -> p b n", n=4), axis=mybir.AxisListType.X)
-        sgc = big("sgc", [128, B], U32)
-        sgs = big("sgs", [128, B], U8)
-        nc.gpsimd.memset(sgc[:], 0)
-        nc.gpsimd.memset(sgs[:], 0)
+        groups = [[0],[1],[2],[3]]
+        sgc = {}
+        sgs = {}
+        for g, cs in enumerate(groups):
+            sgc[g] = big("sgc%d" % g, [128, B], U32)
+            sgs[g] = big("sgs%d" % g, [128, B], U8)
+            nc.gpsimd.memset(sgc[g][:], 0)
+            nc.gpsimd.memset(sgs[g][:].bitcast(U32), 0)
 
         xs = {}
         xg = {}
@@ -92,18 +96,6 @@ def tile_radixsplitattentionpointwise_x1_kernel(tc, x, w, bias, gs, wa, ba, out_
         def load_w(nm):
             nc.sync.dma_start(out=wr[nm][:], in_=wsrc[nm].rearrange("(p j) c -> p j c", j=4))
 
-        load_x(1, 0)
-        load_w("w1")
-        load_x(0, 0)
-        load_w("w0")
-        load_x(1, 1)
-        load_x(0, 1)
-        load_w("a1")
-        load_w("a0")
-        load_x(1, 2)
-        load_x(0, 2)
-        load_x(1, 3)
-        load_x(0, 3)
 
         vec = big("vec", [128, 5, 4], F32)
         bd = big("bd", [128, 4], F32)
@@ -168,18 +160,19 @@ def tile_radixsplitattentionpointwise_x1_kernel(tc, x, w, bias, gs, wa, ba, out_
         u = {}
         dd = {}
         mm = {}
+        oo = {}
         ob = {}
         oc = {}
-        osc = {}
+        osc = big("osc", [128, T], U8)
         for h in range(2):
             k = "%d" % h
             u[0, h] = big("u0" + k, [128, 4, HT], F32)
             u[1, h] = big("u1" + k, [128, 4, HT], F32)
             dd[h] = big("dd" + k, [128, 4, HT], F32)
             mm[h] = big("mm" + k, [128, 4, HT], F32)
+            oo[h] = big("oo" + k, [128, 4, HT], F32)
             ob[h] = big("ob" + k, [128, HT, 4], BF16)
             oc[h] = big("oc" + k, [128, HT], U32)
-            osc[h] = big("osc" + k, [128, HT], U8)
 
         def mx1(r, c):
             for i in range(2):
@@ -247,45 +240,44 @@ def tile_radixsplitattentionpointwise_x1_kernel(tc, x, w, bias, gs, wa, ba, out_
                 nc.tensor.matmul(out=pss[c][:, t, :], lhsT=ut[c][:, t, :], rhs=grp[:], start=True, stop=True)
 
         sgb = {}
-        for h in range(2):
-            sgb[h] = big("sgb%d" % h, [128, HB, 4], BF16)
-
-        def sgate(c):
-            h, o = divmod(c, 2)
-            nc.vector.tensor_mul(
-                out=sgb[h][:, CB * o : CB * (o + 1), :], in0=pss[c][:].rearrange("p t b -> p b t"), in1=gsb[:]
-            )
-
-        def sg_q(h):
-            nc.vector.quantize_mx(
-                out=sgc[:, HB * h : HB * (h + 1)].bitcast(FP8X4),
-                scales=sgs[:, HB * h : HB * (h + 1)],
-                in_=sgb[h][:].rearrange("p b t -> p (b t)"),
-            )
-
         lps = {}
         a0 = {}
-        for h in range(2):
-            a0[h] = big("a0g%d" % h, [128, 4, HB], F32)
+        where = {}
+        for g, cs in enumerate(groups):
+            sgb[g] = big("sgb%d" % g, [128, CB * len(cs), 4], BF16)
+            a0[g] = big("a0g%d" % g, [128, 4, CB * len(cs)], F32)
+            for i, c in enumerate(cs):
+                where[c] = (g, slice(CB * i, CB * (i + 1)))
 
-        def mx2(h):
-            lps[h] = pp.tile([128, 4, B], F32, name="l%d" % h, tag="l", bufs=1)
+        def sgate(c):
+            g, s = where[c]
+            nc.vector.tensor_mul(out=sgb[g][:, s, :], in0=pss[c][:].rearrange("p t b -> p b t"), in1=gsb[:])
+
+        def sg_q(g):
+            k = CB * len(groups[g])
+            nc.vector.quantize_mx(
+                out=sgc[g][:, 0:k].bitcast(FP8X4), scales=sgs[g][:, 0:k], in_=sgb[g][:].rearrange("p b t -> p (b t)")
+            )
+
+        def mx2(g):
+            lps[g] = pp.tile([128, 4, B], F32, name="l%d" % g, tag="l", bufs=1)
             for t in range(4):
                 for i, nm in enumerate(("a0", "a1")):
                     nc.tensor.matmul_mx(
-                        out=lps[h][:, t, :],
+                        out=lps[g][:, t, :],
                         lhsT=wc[nm][:, 128 * t : 128 * (t + 1)].bitcast(FP8X4),
                         lhsT_scale=ws[nm][:, 128 * t : 128 * (t + 1)],
-                        rhs=sgc[:].bitcast(FP8X4),
-                        rhs_scale=sgs[:],
+                        rhs=sgc[g][:].bitcast(FP8X4),
+                        rhs_scale=sgs[g][:],
                         start=(i == 0),
                         stop=(i == 1),
                     )
 
-        def sigm(h):
+        def sigm(g):
+            k = CB * len(groups[g])
             for t in range(4):
                 nc.scalar.activation(
-                    out=a0[h][:, t, :], in_=lps[h][:, t, HB * h : HB * (h + 1)], func=AF.Sigmoid, bias=bd[:, t : t + 1]
+                    out=a0[g][:, t, :], in_=lps[g][:, t, 0:k], func=AF.Sigmoid, bias=bd[:, t : t + 1]
                 )
 
         def blk(c, k2):
@@ -298,21 +290,28 @@ def tile_radixsplitattentionpointwise_x1_kernel(tc, x, w, bias, gs, wa, ba, out_
             nc.vector.tensor_mul(
                 out=mm[h][:, :, s].rearrange("p t (b n) -> p t b n", n=4),
                 in0=dd[h][:, :, s].rearrange("p t (b n) -> p t b n", n=4),
-                in1=a0[h][:, :, CB * o : CB * (o + 1)].unsqueeze(3).to_broadcast([128, 4, CB, 4]),
+                in1=a0[where[c][0]][:, :, where[c][1]].unsqueeze(3).to_broadcast([128, 4, CB, 4]),
             )
 
-        def obf(c, k2):
+        def o_add(c, k2):
             h, o, s = blk(c, k2)
-            nc.vector.tensor_add(
-                out=ob[h][:].rearrange("p (o b k n) t -> p o k b t n", o=2, k=2, n=4)[:, o, k2],
-                in0=mm[h][:, :, s].rearrange("p t (b n) -> p b t n", n=4),
-                in1=u[1, h][:, :, s].rearrange("p t (b n) -> p b t n", n=4),
-            )
+            nc.vector.tensor_add(out=oo[h][:, :, s], in0=mm[h][:, :, s], in1=u[1, h][:, :, s])
 
-        def o_q(h, c0, c1):
-            s = slice(CH * c0, CH * c1)
+        def obf(c, k2, eng):
+            h, o, s = blk(c, k2)
+            dst = ob[h][:].rearrange("p (o b k n) t -> p o k b t n", o=2, k=2, n=4)[:, o, k2]
+            src = oo[h][:, :, s].rearrange("p t (b n) -> p b t n", n=4)
+            if eng == "v":
+                nc.vector.tensor_copy(out=dst, in_=src)
+            else:
+                nc.scalar.copy(out=dst, in_=src)
+
+        def o_q(c):
+            h, o = divmod(c, 2)
+            s = slice(CH * o, CH * (o + 1))
             nc.vector.quantize_mx(
-                out=oc[h][:, s].bitcast(FP8X4), scales=osc[h][:, s], in_=ob[h][:, s, :].rearrange("p k t -> p (k t)")
+                out=oc[h][:, s].bitcast(FP8X4), scales=osc[:, CH * c : CH * (c + 1)],
+                in_=ob[h][:, s, :].rearrange("p k t -> p (k t)")
             )
 
         ops = {}
@@ -323,8 +322,7 @@ def tile_radixsplitattentionpointwise_x1_kernel(tc, x, w, bias, gs, wa, ba, out_
             ps = pp.tile([128, 4, 128], F32, name="o%d%d" % (c, k2), tag=tag, bufs=3 if tag == "z" else 2)
             ops[c, k2] = ps
             for t in range(4):
-                nc.tensor.matmul(out=ps[:, t, :], lhsT=u[1, h][:, t, s], rhs=identf[:], start=True, stop=False, is_transpose=True)
-                nc.tensor.matmul(out=ps[:, t, :], lhsT=mm[h][:, t, s], rhs=identf[:], start=False, stop=True, is_transpose=True)
+                nc.tensor.transpose(ps[:, t, :], oo[h][:, t, s], identf[:])
 
         for c in range(NCH):
             ot[c] = big("ot%d" % c, [128, 2, 128, 4], F32)
@@ -351,133 +349,185 @@ def tile_radixsplitattentionpointwise_x1_kernel(tc, x, w, bias, gs, wa, ba, out_
                     out=out_0[CB * c : CB * (c + 1), 4 * k2 + n, :], in_=ot[c][n::4, k2].rearrange("q p t -> q (p t)")
                 )
 
-        def w_st(h):
-            nc.sync.dma_start(out=words[:, HT * h : HT * (h + 1)], in_=oc[h][:].bitcast(I32))
+        def w_st(c):
+            h, o = divmod(c, 2)
+            nc.sync.dma_start(
+                out=words[:, CH * c : CH * (c + 1)], in_=oc[h][:, CH * o : CH * (o + 1)].bitcast(I32)
+            )
+
+        def s_st(c0, c1):
             for q in range(4):
-                nc.sync.dma_start(
-                    out=srows[4 * q : 4 * q + 4, HT // 4 * h : HT // 4 * (h + 1)],
-                    in_=osc[h][32 * q : 32 * q + 4, :].bitcast(I32),
+                nc.scalar.dma_start(
+                    out=srows[4 * q : 4 * q + 4, CB * 2 * c0 : CB * 2 * c1],
+                    in_=osc[32 * q : 32 * q + 4, CH * c0 : CH * c1].bitcast(I32),
                 )
 
-        w_cp("w1", 2, 4, "s")
+        def warm(i):
+            ps = pp.tile([128, 2, CH], F32, name="warm%d" % i, tag="z", bufs=3)
+            nc.tensor.matmul_mx(
+                out=ps[:].rearrange("p a b -> p (a b)"),
+                lhsT=wc["w1"][:, 0:128].bitcast(FP8X4), lhsT_scale=ws["w1"][:, 0:128],
+                rhs=wc["w1"][:].bitcast(FP8X4), rhs_scale=ws["w1"][:], start=True, stop=True,
+            )
+
+        load_x(1, 0)
+        consts_pe()
+        load_w("w1")
+        w_cp("w1", 0, 2, "s")
+        w_cp("w1", 2, 4, "v")
         x_tr(1, 0)
         x_cp(1, 0, "v")
-        w_cp("w1", 0, 2, "v")
-        x_q(1, 0)
-        consts_pe()
         consts()
-        x_tr(0, 0)
-        w_q("w1", 0, 2)
         w_q("w1", 2, 4)
-        mx1(1, 0)
-        x_cp(0, 0, "s")
-        w_cp("w0", 0, 2, "v")
-        w_q("w0", 0, 2)
-        x_q(0, 0)
-        x_tr(1, 1)
-        x_cp(1, 1, "v")
-        w_cp("w0", 2, 4, "s")
+        x_q(1, 0)
+        load_x(0, 0)
+        x_tr(0, 0)
+        load_x(0, 1)
+        load_w("w0")
         x_tr(0, 1)
+        w_cp("w0", 2, 4, "s")
+        load_x(1, 2)
+        w_q("w1", 0, 2)
+        mx1(1, 0)
         relu(1, 0, "ssss")
-        w_q("w0", 2, 4)
-        mx1(0, 0)
-        relu(0, 0, "ssss")
-        x_q(1, 1)
-        mx1(1, 1)
-        relu(1, 1, "ssss")
-        sum_t(0)
-        x_tr(1, 2)
+        x_cp(0, 0, "v")
         x_cp(0, 1, "v")
+        w_cp("w0", 0, 2, "v")
+        x_q(0, 0)
+        w_q("w0", 0, 2)
+        w_q("w0", 2, 4)
+        load_x(1, 1)
+        x_tr(1, 1)
+        x_cp(1, 1, "s")
         x_q(0, 1)
-        mx1(0, 1)
-        w_cp("a1", 0, 4, "s")
-        w_cp("a0", 0, 4, "v")
-        relu(0, 1, "vvvv")
-        x_tr(0, 2)
-        sum_cp(0, "s")
-        sum_t(1)
-        x_cp(1, 2, "s")
-        w_q("a1", 0, 4)
-        sum_cp(1, "s")
-        x_tr(1, 3)
-        consts2()
-        w_q("a0", 0, 4)
-        x_cp(0, 2, "v")
-        x_cp(1, 3, "s")
-        x_q(1, 2)
-        x_q(0, 2)
-        sum_g(0)
-        sgate(0)
-        sum_g(1)
-        x_q(1, 3)
-        sgate(1)
-        sg_q(0)
-        mx1(1, 2)
-        mx2(0)
-        diff(1)
-        relu(1, 2, "ssss")
-        diff(0)
-        mx1(0, 2)
+        x_tr(1, 2)
+        x_q(1, 1)
+        mx1(0, 0)
+        load_w("a0")
+        load_x(0, 3)
+        load_x(1, 3)
+        relu(0, 0, "vvvv")
+        pass
+        load_w("a1")
         x_tr(0, 3)
-        sigm(0)
-        mul_a(1, 1)
-        mul_a(0, 1)
-        relu(0, 2, "ssss")
-        mul_a(0, 0)
-        sum_t(2)
-        x_cp(0, 3, "s")
+        x_cp(1, 2, "s")
+        x_tr(1, 3)
+        mx1(1, 1)
+        load_x(0, 2)
+        x_cp(0, 3, "v")
+        w_cp("a0", 0, 4, "s")
+        sum_t(0)
+        relu(1, 1, "ssss")
+        w_cp("a1", 0, 4, "v")
+        w_q("a0", 0, 4)
+        x_q(1, 2)
+        mx1(0, 1)
+        relu(0, 1, "ssss")
+        x_tr(0, 2)
+        w_q("a1", 0, 4)
         x_q(0, 3)
-        mul_a(1, 0)
-        diff(2)
-        obf(0, 0)
-        sum_cp(2, "s")
-        obf(1, 0)
+        pass
+        x_cp(0, 2, "v")
+        consts2()
+        sum_t(1)
+        diff(0)
+        mx1(1, 2)
+        x_q(0, 2)
+        sum_cp(0, "s")
+        sum_g(0)
+        sum_cp(1, "s")
+        sum_g(1)
+        sgate(0)
+        relu(1, 2, "sssv")
+        sg_q(0)
+        x_cp(1, 3, "s")
+        x_q(1, 3)
+        mx1(0, 2)
+        relu(0, 2, "ssss")
+        mx2(0)
+        pass
+        sgate(1)
+        diff(1)
         mx1(1, 3)
+        sigm(0)
         relu(1, 3, "ssss")
-        o_tr(0, 1)
+        sum_t(2)
+        sum_cp(2, "s")
         mx1(0, 3)
-        relu(0, 3, "ssss")
-        sum_t(3)
-        diff(3)
-        o_tr(1, 1)
-        obf(0, 1)
-        sum_cp(3, "s")
-        sum_g(2)
-        o_cp(1, 1, "s")
-        o_cp(0, 1, "s")
-        sgate(2)
-        sum_g(3)
-        sgate(3)
         sg_q(1)
         mx2(1)
-        o_tr(1, 0)
+        mul_a(0, 1)
+        mul_a(0, 0)
+        relu(0, 3, "ssss")
+        sum_t(3)
+        o_add(0, 1)
         sigm(1)
-        o_cp(1, 0, "s")
+        sum_g(2)
+        warm(4)
+        obf(0, 1, "s")
+        pass
+        pass
+        sum_cp(3, "s")
+        o_tr(0, 1)
+        o_add(0, 0)
+        o_cp(0, 1, "s")
+        diff(2)
+        diff(3)
+        sgate(2)
+        sum_g(3)
+        mul_a(1, 1)
+        sg_q(2)
+        mx2(2)
+        obf(0, 0, "s")
+        sigm(2)
         o_tr(0, 0)
-        obf(1, 1)
-        o_q(0, 0, 2)
-        w_st(0)
+        mul_a(1, 0)
+        o_add(1, 1)
+        o_tr(1, 1)
         o_cp(0, 0, "s")
-        mul_a(2, 0)
-        o_st(1)
-        o_tr(2, 0)
-        o_st(0)
-        mul_a(3, 0)
-        o_cp(2, 0, "s")
+        sgate(3)
+        o_add(1, 0)
+        sg_q(3)
         mul_a(2, 1)
-        o_tr(3, 0, "z")
-        o_cp(3, 0, "s")
+        mul_a(2, 0)
+        o_cp(1, 1, "s")
+        o_st(0)
+        obf(1, 0, "s")
+        o_add(2, 1)
+        mx2(3)
+        sigm(3)
+        o_add(2, 0)
+        o_tr(1, 0)
+        o_cp(1, 0, "s")
+        o_st(1)
+        obf(1, 1, "s")
+        o_tr(2, 1)
+        o_tr(2, 0)
         mul_a(3, 1)
-        o_tr(3, 1)
-        o_tr(2, 1, "z")
-        o_cp(3, 1, "s")
-        o_st1(3, 1)
-        o_st1(3, 0)
-        obf(3, 0)
+        o_q(0)
+        w_st(0)
+        o_add(3, 1)
+        mul_a(3, 0)
         o_cp(2, 1, "s")
-        obf(3, 1)
-        obf(2, 1)
-        obf(2, 0)
-        o_q(1, 0, 2)
+        o_q(1)
+        o_cp(2, 0, "s")
         o_st(2)
+        o_add(3, 0)
+        obf(3, 1, "v")
+        obf(2, 0, "s")
         w_st(1)
+        obf(3, 0, "v")
+        obf(2, 1, "s")
+        o_tr(3, 1)
+        o_cp(3, 1, "s")
+        o_q(2)
+        o_st1(3, 1)
+        o_q(3)
+        w_st(2)
+        o_tr(3, 0)
+        w_st(3)
+        o_cp(3, 0, "s")
+        pass
+        s_st(0, 4)
+        pass
+        o_st1(3, 0)

@@ -37,13 +37,13 @@ def tile_radixsplitattentionpointwise_x1_kernel(tc, x, w, bias, gs, wa, ba, out_
 
         brow = big("brow", [128, 512], BF16)
         nc.vector.memset(brow[:], 0.0)
+        nc.scalar.dma_start(out=brow[0:2, :], in_=bias)
+        nc.scalar.dma_start(out=brow[2:3, :], in_=gs.unsqueeze(0))
+        nc.scalar.dma_start(out=brow[3:5, :], in_=ba)
         warm = big("warm", [128, 1], F32)
         nc.vector.memset(warm[:], 0.0)
         warm2 = big("warm2", [128, 1], F32)
         nc.scalar.activation(out=warm2[:], in_=warm[:], func=AF.Sigmoid)
-        nc.scalar.dma_start(out=brow[0:2, :], in_=bias)
-        nc.scalar.dma_start(out=brow[2:3, :], in_=gs.unsqueeze(0))
-        nc.scalar.dma_start(out=brow[3:5, :], in_=ba)
 
         identf = big("identf", [128, 128], F32)
         make_identity(nc, identf[:])
@@ -215,7 +215,7 @@ def tile_radixsplitattentionpointwise_x1_kernel(tc, x, w, bias, gs, wa, ba, out_
         ut = {}
         pss = {}
 
-        def sum_t(c):
+        def sum_t(c, plain=0):
             h, o = divmod(c, 2)
             pst[c] = pp.tile([128, 4, 128], F32, name="pst%d" % c, tag="st", bufs=2)
             for t in range(4):
@@ -224,7 +224,7 @@ def tile_radixsplitattentionpointwise_x1_kernel(tc, x, w, bias, gs, wa, ba, out_
                     s = CH * o + 128 * k2
                     nc.tensor.matmul(
                         out=pst[c][:, t, :], lhsT=u[r, h][:, t, s : s + 128], rhs=identf[:],
-                        start=(i == 0), stop=(i == 3), is_transpose=True,
+                        start=(i == 0), stop=(i == 3), is_transpose=(i >= plain),
                     )
 
         def sum_cp(c, eng):
@@ -363,171 +363,169 @@ def tile_radixsplitattentionpointwise_x1_kernel(tc, x, w, bias, gs, wa, ba, out_
                 )
 
         def warm(i):
-            ps = pp.tile([128, 2, CH], F32, name="warm%d" % i, tag="z", bufs=3)
-            nc.tensor.matmul_mx(
-                out=ps[:].rearrange("p a b -> p (a b)"),
-                lhsT=wc["w1"][:, 0:128].bitcast(FP8X4), lhsT_scale=ws["w1"][:, 0:128],
-                rhs=wc["w1"][:].bitcast(FP8X4), rhs_scale=ws["w1"][:], start=True, stop=True,
-            )
+            ps = pp.tile([128, 128], F32, name="pw%d" % i, tag="l", bufs=1)
+            nc.tensor.matmul(out=ps[:], lhsT=identf[:], rhs=identf[:], start=True, stop=True)
 
         load_x(1, 0)
-        consts_pe()
+        warm(3)
         load_w("w1")
-        w_cp("w1", 0, 2, "s")
-        w_cp("w1", 2, 4, "v")
+        consts_pe()
         x_tr(1, 0)
-        x_cp(1, 0, "v")
         consts()
-        w_q("w1", 2, 4)
-        x_q(1, 0)
-        load_x(0, 0)
-        x_tr(0, 0)
-        load_x(0, 1)
-        load_w("w0")
-        x_tr(0, 1)
-        w_cp("w0", 2, 4, "s")
-        load_x(1, 2)
-        w_q("w1", 0, 2)
-        mx1(1, 0)
-        relu(1, 0, "ssss")
-        x_cp(0, 0, "v")
-        x_cp(0, 1, "v")
-        w_cp("w0", 0, 2, "v")
-        x_q(0, 0)
-        w_q("w0", 0, 2)
-        w_q("w0", 2, 4)
-        load_x(1, 1)
-        x_tr(1, 1)
-        x_cp(1, 1, "s")
-        x_q(0, 1)
-        x_tr(1, 2)
-        x_q(1, 1)
-        mx1(0, 0)
-        load_w("a0")
-        load_x(0, 3)
-        load_x(1, 3)
-        relu(0, 0, "vvvv")
-        pass
-        load_w("a1")
-        x_tr(0, 3)
-        x_cp(1, 2, "s")
-        x_tr(1, 3)
-        mx1(1, 1)
-        load_x(0, 2)
-        x_cp(0, 3, "v")
-        w_cp("a0", 0, 4, "s")
-        sum_t(0)
-        relu(1, 1, "ssss")
-        w_cp("a1", 0, 4, "v")
-        w_q("a0", 0, 4)
-        x_q(1, 2)
-        mx1(0, 1)
-        relu(0, 1, "ssss")
-        x_tr(0, 2)
-        w_q("a1", 0, 4)
-        x_q(0, 3)
-        pass
-        x_cp(0, 2, "v")
         consts2()
-        sum_t(1)
-        diff(0)
-        mx1(1, 2)
-        x_q(0, 2)
+        w_cp("w1", 0, 2, "v")
+        warm(0)
+        w_q("w1", 0, 2)
+        load_w("w0")
+        w_cp("w1", 2, 4, "s")
+        load_x(0, 0)
+        w_cp("w0", 2, 4, "v")
+        warm(6)
+        load_x(0, 3)
+        load_x(1, 1)
+        warm(10)
+        x_cp(1, 0, "s")
+        x_q(1, 0)
+        w_q("w1", 2, 4)
+        w_q("w0", 2, 4)
+        x_tr(0, 0)
+        load_x(0, 2)
+        mx1(1, 0)
+        w_cp("w0", 0, 2, "s")
+        w_q("w0", 0, 2)
+        x_cp(0, 0, "s")
+        x_q(0, 0)
+        x_tr(0, 3)
+        x_cp(0, 3, "v")
+        relu(1, 0, "ssss")
+        x_tr(1, 1)
+        x_cp(1, 1, "v")
+        load_x(0, 1)
+        mx1(0, 0)
+        x_q(0, 3)
+        x_q(1, 1)
+        load_x(1, 2)
+        x_tr(0, 1)
+        x_cp(0, 1, "v")
+        x_tr(1, 2)
+        relu(0, 0, "ssss")
+        x_cp(1, 2, "s")
+        load_x(1, 3)
+        x_q(0, 1)
+        load_w("a1")
+        w_cp("a1", 0, 4, "v")
+        mx1(1, 1)
+        sum_t(0, 0)
+        relu(1, 1, "ssss")
+        mx1(0, 1)
+        load_w("a0")
+        x_q(1, 2)
+        w_cp("a0", 0, 4, "v")
+        x_tr(1, 3)
         sum_cp(0, "s")
-        sum_g(0)
-        sum_cp(1, "s")
-        sum_g(1)
-        sgate(0)
-        relu(1, 2, "sssv")
-        sg_q(0)
+        relu(0, 1, "sssv")
+        w_q("a0", 0, 4)
         x_cp(1, 3, "s")
+        x_tr(0, 2)
+        sum_g(0)
+        mx1(1, 2)
         x_q(1, 3)
+        x_cp(0, 2, "s")
+        x_q(0, 2)
+        relu(1, 2, "ssss")
+        sum_t(1, 0)
+        sgate(0)
         mx1(0, 2)
+        w_q("a1", 0, 4)
+        sum_cp(1, "s")
+        sg_q(0)
         relu(0, 2, "ssss")
-        mx2(0)
-        pass
-        sgate(1)
         diff(1)
-        mx1(1, 3)
+        mx2(0)
+        sum_g(1)
         sigm(0)
+        diff(0)
+        mx1(1, 3)
+        sgate(1)
+        sum_t(2, 0)
         relu(1, 3, "ssss")
-        sum_t(2)
-        sum_cp(2, "s")
-        mx1(0, 3)
-        sg_q(1)
-        mx2(1)
-        mul_a(0, 1)
-        mul_a(0, 0)
-        relu(0, 3, "ssss")
-        sum_t(3)
-        o_add(0, 1)
-        sigm(1)
-        sum_g(2)
-        warm(4)
-        obf(0, 1, "s")
-        pass
-        pass
-        sum_cp(3, "s")
-        o_tr(0, 1)
-        o_add(0, 0)
-        o_cp(0, 1, "s")
         diff(2)
-        diff(3)
+        sg_q(1)
+        mul_a(0, 0)
+        warm(11)
+        mul_a(0, 1)
+        mx2(1)
+        o_add(0, 0)
+        o_add(0, 1)
+        mx1(0, 3)
+        sum_cp(2, "s")
+        sigm(1)
+        relu(0, 3, "ssss")
+        mul_a(1, 0)
+        obf(0, 1, "s")
+        sum_g(2)
+        obf(0, 0, "s")
         sgate(2)
-        sum_g(3)
+        warm(13)
+        sum_t(3, 0)
         mul_a(1, 1)
+        sum_cp(3, "s")
         sg_q(2)
         mx2(2)
-        obf(0, 0, "s")
-        sigm(2)
         o_tr(0, 0)
-        mul_a(1, 0)
+        sigm(2)
+        diff(3)
+        o_tr(0, 1)
         o_add(1, 1)
-        o_tr(1, 1)
         o_cp(0, 0, "s")
-        sgate(3)
+        o_cp(0, 1, "s")
         o_add(1, 0)
-        sg_q(3)
-        mul_a(2, 1)
         mul_a(2, 0)
-        o_cp(1, 1, "s")
-        o_st(0)
         obf(1, 0, "s")
-        o_add(2, 1)
-        mx2(3)
-        sigm(3)
-        o_add(2, 0)
+        o_st(0)
+        sum_g(3)
+        sgate(3)
+        warm(12)
+        o_tr(1, 1)
+        o_cp(1, 1, "s")
+        o_q(0)
         o_tr(1, 0)
         o_cp(1, 0, "s")
         o_st(1)
-        obf(1, 1, "s")
-        o_tr(2, 1)
+        warm(7)
+        sg_q(3)
+        mx2(3)
+        mul_a(2, 1)
+        o_add(2, 0)
         o_tr(2, 0)
-        mul_a(3, 1)
-        o_q(0)
+        o_add(2, 1)
+        o_tr(2, 1)
         w_st(0)
-        o_add(3, 1)
+        sigm(3)
         mul_a(3, 0)
-        o_cp(2, 1, "s")
+        obf(1, 1, "s")
+        warm(2)
         o_q(1)
         o_cp(2, 0, "s")
-        o_st(2)
+        warm(9)
         o_add(3, 0)
-        obf(3, 1, "v")
-        obf(2, 0, "s")
+        o_tr(3, 0)
         w_st(1)
-        obf(3, 0, "v")
+        mul_a(3, 1)
+        o_cp(2, 1, "s")
         obf(2, 1, "s")
+        o_st(2)
+        o_add(3, 1)
+        obf(2, 0, "v")
+        o_cp(3, 0, "s")
+        o_st1(3, 0)
+        obf(3, 0, "v")
+        o_q(2)
+        w_st(2)
+        obf(3, 1, "s")
         o_tr(3, 1)
         o_cp(3, 1, "s")
-        o_q(2)
-        o_st1(3, 1)
         o_q(3)
-        w_st(2)
-        o_tr(3, 0)
         w_st(3)
-        o_cp(3, 0, "s")
-        pass
+        o_st1(3, 1)
         s_st(0, 4)
-        pass
-        o_st1(3, 0)

@@ -21,8 +21,6 @@ FLOPS = 2 * R * T * C * E + 2 * R * B * E * E
 CH = 256
 CB = CH // N
 NCH = T // CH
-HB = 64
-HT = HB * N
 
 
 def tile_radixsplitattentionpointwise_x1_kernel(tc, x, w, bias, gs, wa, ba, out_0, out_1, out_2):
@@ -40,30 +38,24 @@ def tile_radixsplitattentionpointwise_x1_kernel(tc, x, w, bias, gs, wa, ba, out_
         nc.scalar.dma_start(out=brow[0:2, :], in_=bias)
         nc.scalar.dma_start(out=brow[2:3, :], in_=gs.unsqueeze(0))
         nc.scalar.dma_start(out=brow[3:5, :], in_=ba)
-        warm = big("warm", [128, 1], F32)
-        nc.vector.memset(warm[:], 0.0)
-        warm2 = big("warm2", [128, 1], F32)
-        nc.scalar.activation(out=warm2[:], in_=warm[:], func=AF.Sigmoid)
+        zero = big("zero", [128, 1], F32)
+        nc.vector.memset(zero[:], 0.0)
+        half = big("half", [128, 1], F32)
+        nc.scalar.activation(out=half[:], in_=zero[:], func=AF.Sigmoid)
 
         identf = big("identf", [128, 128], F32)
         make_identity(nc, identf[:])
-        perm = big("perm", [128, 128], F32)
-        nc.vector.tensor_copy(
-            out=perm[:].rearrange("p (k b h) -> p k b h", k=2, h=2),
-            in_=identf[:].rearrange("p (b k h) -> p k b h", k=2, h=2),
-        )
         identb = big("identb", [128, 128], BF16)
         nc.vector.tensor_copy(out=identb[:], in_=identf[:])
         grp = big("grp", [128, CB], F32)
         nc.vector.reduce_sum(out=grp[:], in_=identf[:].rearrange("p (b n) -> p b n", n=4), axis=mybir.AxisListType.X)
-        groups = [[0],[1],[2],[3]]
         sgc = {}
         sgs = {}
-        for g, cs in enumerate(groups):
-            sgc[g] = big("sgc%d" % g, [128, B], U32)
-            sgs[g] = big("sgs%d" % g, [128, B], U8)
-            nc.gpsimd.memset(sgc[g][:], 0)
-            nc.gpsimd.memset(sgs[g][:].bitcast(U32), 0)
+        for c in range(NCH):
+            sgc[c] = big("sgc%d" % c, [128, B], U32)
+            sgs[c] = big("sgs%d" % c, [128, B], U8)
+            nc.gpsimd.memset(sgc[c][:], 0)
+            nc.gpsimd.memset(sgs[c][:].bitcast(U32), 0)
 
         xs = {}
         xg = {}
@@ -96,7 +88,6 @@ def tile_radixsplitattentionpointwise_x1_kernel(tc, x, w, bias, gs, wa, ba, out_
         def load_w(nm):
             nc.sync.dma_start(out=wr[nm][:], in_=wsrc[nm].rearrange("(p j) c -> p j c", j=4))
 
-
         vec = big("vec", [128, 5, 4], F32)
         bd = big("bd", [128, 4], F32)
         gsb = big("gsb", [128, CB, 4], F32)
@@ -110,9 +101,9 @@ def tile_radixsplitattentionpointwise_x1_kernel(tc, x, w, bias, gs, wa, ba, out_
             nc.vector.tensor_copy(out=vec[:], in_=ct[:, :, 0:5].rearrange("p t r -> p r t"))
 
         def consts2():
-            nc.vector.tensor_sub(out=bd[:], in0=vec[:, 3, :], in1=vec[:, 4, :])
-            nc.vector.tensor_scalar(
-                out=gsb[:], in0=vec[:, 2:3, :].to_broadcast([128, CB, 4]), scalar1=0.125, scalar2=None, op0=MUL
+            nc.gpsimd.tensor_sub(out=bd[:], in0=vec[:, 3, :], in1=vec[:, 4, :])
+            nc.gpsimd.tensor_scalar(
+                out=gsb[:], in0=vec[:, 2:3, :].to_broadcast([128, CB, 4]), scalar1=half[:], scalar2=0.25, op0=MUL, op1=MUL
             )
 
         xt = {}
@@ -123,11 +114,11 @@ def tile_radixsplitattentionpointwise_x1_kernel(tc, x, w, bias, gs, wa, ba, out_
             words = xs[r, c][:].bitcast(F32)
             for j in range(2):
                 for u in range(2):
-                    nc.tensor.transpose(ps[:, j, u, :], words[:, 256 * j + u : 256 * (j + 1) : 2], perm[:])
+                    nc.tensor.transpose(ps[:, j, u, :], words[:, 256 * j + u : 256 * (j + 1) : 2], identf[:])
 
         def x_cp(r, c, eng):
-            dst = xg[r, c][:].bitcast(F32).rearrange("p (q j u) -> p q j u", j=2, u=2)
-            src = xt[r, c][:].rearrange("p j u q -> p q j u")
+            dst = xg[r, c][:].bitcast(F32).rearrange("p (j q u) -> p j q u", j=2, u=2)
+            src = xt[r, c][:].rearrange("p j u q -> p j q u")
             if eng == "v":
                 nc.vector.tensor_copy(out=dst, in_=src)
             else:
@@ -163,16 +154,18 @@ def tile_radixsplitattentionpointwise_x1_kernel(tc, x, w, bias, gs, wa, ba, out_
         oo = {}
         ob = {}
         oc = {}
+        ot = {}
+        for c in range(NCH):
+            k = "%d" % c
+            u[0, c] = big("u0" + k, [128, 2, 4, 128], F32)
+            u[1, c] = big("u1" + k, [128, 2, 4, 128], F32)
+            dd[c] = big("dd" + k, [128, 2, 4, 128], F32)
+            mm[c] = big("mm" + k, [128, 2, 4, 128], F32)
+            oo[c] = big("oo" + k, [128, 2, 4, 128], F32)
+            ob[c] = big("ob" + k, [128, CH * 4], BF16)
+            oc[c] = big("oc" + k, [128, CH], U32)
+            ot[c] = big("ot" + k, [128, 2, 128, 4], F32)
         osc = big("osc", [128, T], U8)
-        for h in range(2):
-            k = "%d" % h
-            u[0, h] = big("u0" + k, [128, 4, HT], F32)
-            u[1, h] = big("u1" + k, [128, 4, HT], F32)
-            dd[h] = big("dd" + k, [128, 4, HT], F32)
-            mm[h] = big("mm" + k, [128, 4, HT], F32)
-            oo[h] = big("oo" + k, [128, 4, HT], F32)
-            ob[h] = big("ob" + k, [128, HT, 4], BF16)
-            oc[h] = big("oc" + k, [128, HT], U32)
 
         def mx1(r, c):
             for i in range(2):
@@ -190,40 +183,29 @@ def tile_radixsplitattentionpointwise_x1_kernel(tc, x, w, bias, gs, wa, ba, out_
                         stop=True,
                     )
 
-        def cols(c):
-            h, o = divmod(c, 2)
-            return h, slice(CH * o, CH * (o + 1))
-
         def relu(r, c, eng="ssss"):
-            h, s = cols(c)
             for t in range(4):
+                src = z[r, c, t // 2][:, t % 2, :].rearrange("p (j q) -> p j q", j=2)
                 if eng[t] == "s":
-                    nc.scalar.activation(
-                        out=u[r, h][:, t, s], in_=z[r, c, t // 2][:, t % 2, :], func=AF.Relu, bias=vec[:, r, t : t + 1]
-                    )
+                    nc.scalar.activation(out=u[r, c][:, :, t, :], in_=src, func=AF.Relu, bias=vec[:, r, t : t + 1])
                 else:
                     nc.vector.tensor_scalar(
-                        out=u[r, h][:, t, s], in0=z[r, c, t // 2][:, t % 2, :], scalar1=vec[:, r, t : t + 1],
-                        scalar2=0.0, op0=ADD, op1=MAX,
+                        out=u[r, c][:, :, t, :], in0=src, scalar1=vec[:, r, t : t + 1], scalar2=0.0, op0=ADD, op1=MAX
                     )
 
         def diff(c):
-            h, s = cols(c)
-            nc.vector.tensor_sub(out=dd[h][:, :, s], in0=u[0, h][:, :, s], in1=u[1, h][:, :, s])
+            nc.vector.tensor_sub(out=dd[c][:], in0=u[0, c][:], in1=u[1, c][:])
 
         pst = {}
         ut = {}
         pss = {}
 
         def sum_t(c, plain=0):
-            h, o = divmod(c, 2)
             pst[c] = pp.tile([128, 4, 128], F32, name="pst%d" % c, tag="st", bufs=2)
             for t in range(4):
                 for i in range(4):
-                    r, k2 = 1 - i // 2, i % 2
-                    s = CH * o + 128 * k2
                     nc.tensor.matmul(
-                        out=pst[c][:, t, :], lhsT=u[r, h][:, t, s : s + 128], rhs=identf[:],
+                        out=pst[c][:, t, :], lhsT=u[1 - i // 2, c][:, i % 2, t, :], rhs=identf[:],
                         start=(i == 0), stop=(i == 3), is_transpose=(i >= plain),
                     )
 
@@ -242,290 +224,240 @@ def tile_radixsplitattentionpointwise_x1_kernel(tc, x, w, bias, gs, wa, ba, out_
         sgb = {}
         lps = {}
         a0 = {}
-        where = {}
-        for g, cs in enumerate(groups):
-            sgb[g] = big("sgb%d" % g, [128, CB * len(cs), 4], BF16)
-            a0[g] = big("a0g%d" % g, [128, 4, CB * len(cs)], F32)
-            for i, c in enumerate(cs):
-                where[c] = (g, slice(CB * i, CB * (i + 1)))
+        for c in range(NCH):
+            sgb[c] = big("sgb%d" % c, [128, CB, 4], BF16)
+            a0[c] = big("a0g%d" % c, [128, 4, CB], F32)
 
         def sgate(c):
-            g, s = where[c]
-            nc.vector.tensor_mul(out=sgb[g][:, s, :], in0=pss[c][:].rearrange("p t b -> p b t"), in1=gsb[:])
+            nc.vector.tensor_mul(out=sgb[c][:], in0=pss[c][:].rearrange("p t b -> p b t"), in1=gsb[:])
 
-        def sg_q(g):
-            k = CB * len(groups[g])
+        def sg_q(c):
             nc.vector.quantize_mx(
-                out=sgc[g][:, 0:k].bitcast(FP8X4), scales=sgs[g][:, 0:k], in_=sgb[g][:].rearrange("p b t -> p (b t)")
+                out=sgc[c][:, 0:CB].bitcast(FP8X4), scales=sgs[c][:, 0:CB], in_=sgb[c][:].rearrange("p b t -> p (b t)")
             )
 
-        def mx2(g):
-            lps[g] = pp.tile([128, 4, B], F32, name="l%d" % g, tag="l", bufs=1)
+        def mx2(c):
+            lps[c] = pp.tile([128, 4, B], F32, name="l%d" % c, tag="l", bufs=1)
             for t in range(4):
                 for i, nm in enumerate(("a0", "a1")):
                     nc.tensor.matmul_mx(
-                        out=lps[g][:, t, :],
+                        out=lps[c][:, t, :],
                         lhsT=wc[nm][:, 128 * t : 128 * (t + 1)].bitcast(FP8X4),
                         lhsT_scale=ws[nm][:, 128 * t : 128 * (t + 1)],
-                        rhs=sgc[g][:].bitcast(FP8X4),
-                        rhs_scale=sgs[g][:],
+                        rhs=sgc[c][:].bitcast(FP8X4),
+                        rhs_scale=sgs[c][:],
                         start=(i == 0),
                         stop=(i == 1),
                     )
 
-        def sigm(g):
-            k = CB * len(groups[g])
+        def sigm(c):
             for t in range(4):
-                nc.scalar.activation(
-                    out=a0[g][:, t, :], in_=lps[g][:, t, 0:k], func=AF.Sigmoid, bias=bd[:, t : t + 1]
-                )
+                nc.scalar.activation(out=a0[c][:, t, :], in_=lps[c][:, t, 0:CB], func=AF.Sigmoid, bias=bd[:, t : t + 1])
 
-        def blk(c, k2):
-            h, o = divmod(c, 2)
-            s = CH * o + 128 * k2
-            return h, o, slice(s, s + 128)
-
-        def mul_a(c, k2):
-            h, o, s = blk(c, k2)
+        def mul_a(c, j):
             nc.vector.tensor_mul(
-                out=mm[h][:, :, s].rearrange("p t (b n) -> p t b n", n=4),
-                in0=dd[h][:, :, s].rearrange("p t (b n) -> p t b n", n=4),
-                in1=a0[where[c][0]][:, :, where[c][1]].unsqueeze(3).to_broadcast([128, 4, CB, 4]),
+                out=mm[c][:, j].rearrange("p t (b i) -> p t b i", i=4),
+                in0=dd[c][:, j].rearrange("p t (b i) -> p t b i", i=4),
+                in1=a0[c][:].unsqueeze(3).to_broadcast([128, 4, CB, 4]),
             )
 
-        def o_add(c, k2):
-            h, o, s = blk(c, k2)
-            nc.vector.tensor_add(out=oo[h][:, :, s], in0=mm[h][:, :, s], in1=u[1, h][:, :, s])
+        def o_add(c, j):
+            nc.vector.tensor_add(out=oo[c][:, j], in0=mm[c][:, j], in1=u[1, c][:, j])
 
-        def obf(c, k2, eng):
-            h, o, s = blk(c, k2)
-            dst = ob[h][:].rearrange("p (o b k n) t -> p o k b t n", o=2, k=2, n=4)[:, o, k2]
-            src = oo[h][:, :, s].rearrange("p t (b n) -> p b t n", n=4)
+        def obf(c, eng):
+            dst = ob[c][:].rearrange("p (q i k) -> p q k i", i=2, k=8)
+            src = oo[c][:].rearrange("p j t q -> p (j t) q").rearrange("p k (q i) -> p q k i", i=2)
             if eng == "v":
                 nc.vector.tensor_copy(out=dst, in_=src)
             else:
                 nc.scalar.copy(out=dst, in_=src)
 
         def o_q(c):
-            h, o = divmod(c, 2)
-            s = slice(CH * o, CH * (o + 1))
-            nc.vector.quantize_mx(
-                out=oc[h][:, s].bitcast(FP8X4), scales=osc[:, CH * c : CH * (c + 1)],
-                in_=ob[h][:, s, :].rearrange("p k t -> p (k t)")
-            )
+            nc.vector.quantize_mx(out=oc[c][:].bitcast(FP8X4), scales=osc[:, CH * c : CH * (c + 1)], in_=ob[c][:])
 
         ops = {}
-        ot = {}
 
-        def o_tr(c, k2, tag="tp"):
-            h, o, s = blk(c, k2)
-            ps = pp.tile([128, 4, 128], F32, name="o%d%d" % (c, k2), tag=tag, bufs=3 if tag == "z" else 2)
-            ops[c, k2] = ps
+        def o_tr(c, j, tag="tp"):
+            ps = pp.tile([128, 4, 128], F32, name="o%d%d" % (c, j), tag=tag, bufs=3 if tag == "z" else 2)
+            ops[c, j] = ps
             for t in range(4):
-                nc.tensor.transpose(ps[:, t, :], oo[h][:, t, s], identf[:])
+                nc.tensor.transpose(ps[:, t, :], oo[c][:, j, t, :], identf[:])
 
-        for c in range(NCH):
-            ot[c] = big("ot%d" % c, [128, 2, 128, 4], F32)
-
-        def o_cp(c, k2, eng):
-            src = ops[c, k2][:].rearrange("q t p -> q p t")
+        def o_cp(c, j, eng):
+            src = ops[c, j][:].rearrange("q t p -> q p t")
             if eng == "v":
-                nc.vector.tensor_copy(out=ot[c][:, k2], in_=src)
+                nc.vector.tensor_copy(out=ot[c][:, j], in_=src)
             else:
-                nc.scalar.copy(out=ot[c][:, k2], in_=src)
+                nc.scalar.copy(out=ot[c][:, j], in_=src)
 
+        rows = out_0.rearrange("b n e -> (b n) e").rearrange("(c q j) e -> c q j e", c=NCH, j=2)
         words = out_1.rearrange("g p m t -> (g p) (m t)").bitcast(I32)
         srows = out_2.rearrange("g q m -> (g q) m").bitcast(I32)
 
         def o_st(c):
-            for n in range(4):
-                nc.sync.dma_start(
-                    out=out_0[CB * c : CB * (c + 1), n::4, :], in_=ot[c][n::4].rearrange("q k p t -> q k (p t)")
-                )
+            nc.sync.dma_start(
+                out=rows[c].rearrange("q j e -> q (j e)"), in_=ot[c][:].rearrange("q j p t -> q (j p t)")
+            )
 
-        def o_st1(c, k2):
-            for n in range(4):
-                nc.sync.dma_start(
-                    out=out_0[CB * c : CB * (c + 1), 4 * k2 + n, :], in_=ot[c][n::4, k2].rearrange("q p t -> q (p t)")
-                )
+        def o_st1(c, j):
+            nc.sync.dma_start(out=rows[c, :, j, :], in_=ot[c][:, j].rearrange("q p t -> q (p t)"))
 
         def w_st(c):
-            h, o = divmod(c, 2)
-            nc.sync.dma_start(
-                out=words[:, CH * c : CH * (c + 1)], in_=oc[h][:, CH * o : CH * (o + 1)].bitcast(I32)
-            )
+            nc.sync.dma_start(out=words[:, CH * c : CH * (c + 1)], in_=oc[c][:].bitcast(I32))
 
         def s_st(c0, c1):
             for q in range(4):
                 nc.scalar.dma_start(
-                    out=srows[4 * q : 4 * q + 4, CB * 2 * c0 : CB * 2 * c1],
+                    out=srows[4 * q : 4 * q + 4, CH // 4 * c0 : CH // 4 * c1],
                     in_=osc[32 * q : 32 * q + 4, CH * c0 : CH * c1].bitcast(I32),
                 )
 
-        def warm(i):
-            ps = pp.tile([128, 128], F32, name="pw%d" % i, tag="l", bufs=1)
-            nc.tensor.matmul(out=ps[:], lhsT=identf[:], rhs=identf[:], start=True, stop=True)
-
         load_x(1, 0)
-        warm(3)
-        load_w("w1")
-        consts_pe()
         x_tr(1, 0)
-        consts()
-        consts2()
-        w_cp("w1", 0, 2, "v")
-        warm(0)
-        w_q("w1", 0, 2)
-        load_w("w0")
-        w_cp("w1", 2, 4, "s")
         load_x(0, 0)
-        w_cp("w0", 2, 4, "v")
-        warm(6)
-        load_x(0, 3)
-        load_x(1, 1)
-        warm(10)
         x_cp(1, 0, "s")
-        x_q(1, 0)
-        w_q("w1", 2, 4)
-        w_q("w0", 2, 4)
+        load_x(0, 3)
         x_tr(0, 0)
-        load_x(0, 2)
-        mx1(1, 0)
-        w_cp("w0", 0, 2, "s")
-        w_q("w0", 0, 2)
-        x_cp(0, 0, "s")
-        x_q(0, 0)
         x_tr(0, 3)
-        x_cp(0, 3, "v")
-        relu(1, 0, "ssss")
-        x_tr(1, 1)
-        x_cp(1, 1, "v")
+        load_w("w1")
+        x_q(1, 0)
+        load_w("w0")
+        load_x(1, 1)
+        consts_pe()
+        w_cp("w1", 2, 4, "s")
+        load_x(1, 2)
         load_x(0, 1)
+        x_cp(0, 0, "s")
+        load_x(1, 3)
+        w_cp("w0", 0, 2, "s")
+        w_cp("w1", 0, 2, "v")
+        w_q("w1", 0, 2)
+        x_cp(0, 3, "v")
+        w_q("w1", 2, 4)
+        mx1(1, 0)
+        x_tr(1, 1)
+        x_tr(1, 2)
+        consts()
+        x_q(0, 0)
+        w_cp("w0", 2, 4, "v")
+        w_q("w0", 0, 2)
+        w_q("w0", 2, 4)
+        relu(1, 0, "sssv")
+        x_cp(1, 1, "s")
         mx1(0, 0)
+        load_w("a0")
         x_q(0, 3)
         x_q(1, 1)
-        load_x(1, 2)
         x_tr(0, 1)
-        x_cp(0, 1, "v")
-        x_tr(1, 2)
         relu(0, 0, "ssss")
-        x_cp(1, 2, "s")
-        load_x(1, 3)
-        x_q(0, 1)
-        load_w("a1")
-        w_cp("a1", 0, 4, "v")
+        x_cp(0, 1, "s")
+        x_cp(1, 2, "v")
+        w_cp("a0", 0, 4, "v")
+        load_x(0, 2)
+        diff(0)
         mx1(1, 1)
+        x_q(0, 1)
         sum_t(0, 0)
         relu(1, 1, "ssss")
-        mx1(0, 1)
-        load_w("a0")
-        x_q(1, 2)
-        w_cp("a0", 0, 4, "v")
-        x_tr(1, 3)
-        sum_cp(0, "s")
-        relu(0, 1, "sssv")
-        w_q("a0", 0, 4)
-        x_cp(1, 3, "s")
         x_tr(0, 2)
+        x_q(1, 2)
+        load_w("a1")
+        w_cp("a1", 0, 4, "v")
+        x_tr(1, 3)
+        w_q("a0", 0, 4)
+        sum_cp(0, "s")
+        consts2()
+        x_cp(0, 2, "s")
+        w_q("a1", 0, 4)
+        mx1(0, 1)
+        relu(0, 1, "ssss")
+        x_cp(1, 3, "s")
+        x_q(0, 2)
         sum_g(0)
         mx1(1, 2)
-        x_q(1, 3)
-        x_cp(0, 2, "s")
-        x_q(0, 2)
+        sgate(0)
         relu(1, 2, "ssss")
         sum_t(1, 0)
-        sgate(0)
-        mx1(0, 2)
-        w_q("a1", 0, 4)
-        sum_cp(1, "s")
+        x_q(1, 3)
         sg_q(0)
+        mx1(0, 2)
+        sum_cp(1, "v")
         relu(0, 2, "ssss")
-        diff(1)
         mx2(0)
-        sum_g(1)
         sigm(0)
-        diff(0)
-        mx1(1, 3)
+        diff(1)
+        sum_g(1)
         sgate(1)
-        sum_t(2, 0)
-        relu(1, 3, "ssss")
+        mx1(1, 3)
         diff(2)
+        sum_t(2, 0)
         sg_q(1)
-        mul_a(0, 0)
-        warm(11)
-        mul_a(0, 1)
         mx2(1)
-        o_add(0, 0)
-        o_add(0, 1)
-        mx1(0, 3)
+        relu(1, 3, "ssss")
+        mul_a(0, 0)
         sum_cp(2, "s")
+        mx1(0, 3)
+        mul_a(0, 1)
         sigm(1)
+        o_add(0, 0)
         relu(0, 3, "ssss")
-        mul_a(1, 0)
-        obf(0, 1, "s")
         sum_g(2)
-        obf(0, 0, "s")
-        sgate(2)
-        warm(13)
-        sum_t(3, 0)
+        o_add(0, 1)
         mul_a(1, 1)
-        sum_cp(3, "s")
+        sum_t(3, 0)
+        sgate(2)
+        mul_a(1, 0)
+        obf(0, "s")
         sg_q(2)
-        mx2(2)
-        o_tr(0, 0)
-        sigm(2)
-        diff(3)
+        sum_cp(3, "s")
         o_tr(0, 1)
-        o_add(1, 1)
-        o_cp(0, 0, "s")
+        o_tr(0, 0)
         o_cp(0, 1, "s")
+        diff(3)
+        o_add(1, 1)
+        mx2(2)
+        sigm(2)
+        o_cp(0, 0, "s")
+        sum_g(3)
         o_add(1, 0)
         mul_a(2, 0)
-        obf(1, 0, "s")
         o_st(0)
-        sum_g(3)
         sgate(3)
-        warm(12)
-        o_tr(1, 1)
-        o_cp(1, 1, "s")
+        obf(1, "s")
         o_q(0)
         o_tr(1, 0)
+        o_tr(1, 1)
         o_cp(1, 0, "s")
-        o_st(1)
-        warm(7)
         sg_q(3)
         mx2(3)
         mul_a(2, 1)
+        o_cp(1, 1, "s")
+        o_st(1)
         o_add(2, 0)
-        o_tr(2, 0)
-        o_add(2, 1)
-        o_tr(2, 1)
         w_st(0)
+        o_add(2, 1)
         sigm(3)
-        mul_a(3, 0)
-        obf(1, 1, "s")
-        warm(2)
+        obf(2, "s")
         o_q(1)
-        o_cp(2, 0, "s")
-        warm(9)
-        o_add(3, 0)
-        o_tr(3, 0)
         w_st(1)
+        mul_a(3, 0)
         mul_a(3, 1)
-        o_cp(2, 1, "s")
-        obf(2, 1, "s")
-        o_st(2)
+        o_add(3, 0)
+        o_tr(2, 0)
+        o_cp(2, 0, "s")
+        o_q(2)
         o_add(3, 1)
-        obf(2, 0, "v")
+        o_tr(2, 1)
+        o_cp(2, 1, "s")
+        w_st(2)
+        obf(3, "v")
+        o_st(2)
+        o_tr(3, 0)
         o_cp(3, 0, "s")
         o_st1(3, 0)
-        obf(3, 0, "v")
-        o_q(2)
-        w_st(2)
-        obf(3, 1, "s")
-        o_tr(3, 1)
-        o_cp(3, 1, "s")
         o_q(3)
         w_st(3)
-        o_st1(3, 1)
+        o_tr(3, 1)
+        o_cp(3, 1, "s")
         s_st(0, 4)
+        o_st1(3, 1)

from contextlib import ExitStack

import concourse.mybir as mybir
from concourse.masks import make_identity

F32 = mybir.dt.float32
BF16 = mybir.dt.bfloat16
U32 = mybir.dt.uint32
I32 = mybir.dt.int32
U8 = mybir.dt.uint8
FP8X4 = mybir.dt.float8_e4m3fn_x4
ADD = mybir.AluOpType.add
MUL = mybir.AluOpType.mult
MAX = mybir.AluOpType.max
AF = mybir.ActivationFunctionType

R, B, N, C, E = 2, 128, 8, 512, 512
T = B * N
FLOPS = 2 * R * T * C * E + 2 * R * B * E * E

CH = 256
CB = CH // N
NCH = T // CH


def tile_radixsplitattentionpointwise_x1_kernel(tc, x, w, bias, gs, wa, ba, out_0, out_1, out_2):
    nc = tc.nc
    with ExitStack() as ctx:
        sb = ctx.enter_context(tc.tile_pool(name="sb", bufs=1))
        pp = ctx.enter_context(tc.psum_pool(name="pp", bufs=1))
        ctx.enter_context(tc.manual_schedule())

        def big(name, shape, dtype):
            return sb.tile(shape, dtype, name=name, align_bytes=64)

        brow = big("brow", [128, 512], BF16)
        nc.vector.memset(brow[:], 0.0)
        nc.scalar.dma_start(out=brow[0:2, :], in_=bias)
        nc.scalar.dma_start(out=brow[2:3, :], in_=gs.unsqueeze(0))
        nc.scalar.dma_start(out=brow[3:5, :], in_=ba)
        zero = big("zero", [128, 1], F32)
        nc.vector.memset(zero[:], 0.0)
        half = big("half", [128, 1], F32)
        nc.scalar.activation(out=half[:], in_=zero[:], func=AF.Sigmoid)

        identf = big("identf", [128, 128], F32)
        make_identity(nc, identf[:])
        identb = big("identb", [128, 128], BF16)
        nc.vector.tensor_copy(out=identb[:], in_=identf[:])
        grp = big("grp", [128, CB], F32)
        nc.vector.reduce_sum(out=grp[:], in_=identf[:].rearrange("p (b n) -> p b n", n=4), axis=mybir.AxisListType.X)
        sgc = {}
        sgs = {}
        for c in range(NCH):
            sgc[c] = big("sgc%d" % c, [128, B], U32)
            sgs[c] = big("sgs%d" % c, [128, B], U8)
            nc.gpsimd.memset(sgc[c][:], 0)
            nc.gpsimd.memset(sgs[c][:].bitcast(U32), 0)

        xs = {}
        xg = {}
        xc = {}
        xsc = {}
        for c in range(NCH):
            for r in range(R):
                k = "%d%d" % (r, c)
                xs[r, c] = big("xs" + k, [128, 1024], BF16)
                xg[r, c] = big("xg" + k, [128, 1024], BF16)
                xc[r, c] = big("xc" + k, [128, CH], U32)
                xsc[r, c] = big("xsc" + k, [128, CH], U8)
        wr = {}
        wg = {}
        wc = {}
        ws = {}
        for nm in ("w1", "w0", "a1", "a0"):
            wr[nm] = big("wr" + nm, [128, 4, 512], BF16)
            wg[nm] = big("wg" + nm, [128, 2048], BF16)
            wc[nm] = big("wc" + nm, [128, 512], U32)
            ws[nm] = big("ws" + nm, [128, 512], U8)
        wsrc = {"w0": w[0], "w1": w[1], "a0": wa[0], "a1": wa[1]}

        def load_x(r, c):
            nc.sync.dma_start(
                out=xs[r, c][:],
                in_=x[r, CB * c : CB * (c + 1)].rearrange("b n c -> (b n) c").rearrange("(q j) c -> q (j c)", j=2),
            )

        def load_w(nm):
            nc.sync.dma_start(out=wr[nm][:], in_=wsrc[nm].rearrange("(p j) c -> p j c", j=4))

        vec = big("vec", [128, 5, 4], F32)
        bd = big("bd", [128, 4], F32)
        gsb = big("gsb", [128, CB, 4], F32)
        ct = pp.tile([128, 4, 128], BF16, name="ct", tag="st", bufs=2)

        def consts_pe():
            for t in range(4):
                nc.tensor.transpose(ct[:, t, :], brow[:, t::4], identb[:])

        def consts():
            nc.vector.tensor_copy(out=vec[:], in_=ct[:, :, 0:5].rearrange("p t r -> p r t"))

        def consts2():
            nc.gpsimd.tensor_sub(out=bd[:], in0=vec[:, 3, :], in1=vec[:, 4, :])
            nc.gpsimd.tensor_scalar(
                out=gsb[:], in0=vec[:, 2:3, :].to_broadcast([128, CB, 4]), scalar1=half[:], scalar2=0.25, op0=MUL, op1=MUL
            )

        xt = {}

        def x_tr(r, c):
            ps = pp.tile([128, 2, 2, 128], F32, name="xt%d%d" % (r, c), tag="tp", bufs=2)
            xt[r, c] = ps
            words = xs[r, c][:].bitcast(F32)
            for j in range(2):
                for u in range(2):
                    nc.tensor.transpose(ps[:, j, u, :], words[:, 256 * j + u : 256 * (j + 1) : 2], identf[:])

        def x_cp(r, c, eng):
            dst = xg[r, c][:].bitcast(F32).rearrange("p (j q u) -> p j q u", j=2, u=2)
            src = xt[r, c][:].rearrange("p j u q -> p j q u")
            if eng == "v":
                nc.vector.tensor_copy(out=dst, in_=src)
            else:
                nc.scalar.copy(out=dst, in_=src)

        def x_q(r, c):
            nc.vector.quantize_mx(out=xc[r, c][:].bitcast(FP8X4), scales=xsc[r, c][:], in_=xg[r, c][:])

        def w_cp(nm, t0, t1, eng):
            dst = wg[nm][:].rearrange("p (t m j) -> p t m j", t=4, j=4)[:, t0:t1]
            src = wr[nm][:].rearrange("p j (m t) -> p t m j", t=4)[:, t0:t1]
            if eng == "v":
                if nm == "a1":
                    nc.vector.tensor_scalar(out=dst, in0=src, scalar1=-1.0, scalar2=None, op0=MUL)
                else:
                    nc.vector.tensor_copy(out=dst, in_=src)
            elif nm == "a1":
                nc.scalar.activation(out=dst, in_=src, func=AF.Copy, scale=-1.0)
            else:
                nc.scalar.copy(out=dst, in_=src)

        def w_q(nm, t0, t1):
            nc.vector.quantize_mx(
                out=wc[nm][:, 128 * t0 : 128 * t1].bitcast(FP8X4),
                scales=ws[nm][:, 128 * t0 : 128 * t1],
                in_=wg[nm][:, 512 * t0 : 512 * t1],
            )

        z = {}
        u = {}
        dd = {}
        mm = {}
        oo = {}
        ob = {}
        oc = {}
        ot = {}
        for c in range(NCH):
            k = "%d" % c
            u[0, c] = big("u0" + k, [128, 2, 4, 128], F32)
            u[1, c] = big("u1" + k, [128, 2, 4, 128], F32)
            dd[c] = big("dd" + k, [128, 2, 4, 128], F32)
            mm[c] = big("mm" + k, [128, 2, 4, 128], F32)
            oo[c] = big("oo" + k, [128, 2, 4, 128], F32)
            ob[c] = big("ob" + k, [128, CH * 4], BF16)
            oc[c] = big("oc" + k, [128, CH], U32)
            ot[c] = big("ot" + k, [128, 2, 128, 4], F32)
        osc = big("osc", [128, T], U8)

        def mx1(r, c):
            for i in range(2):
                ps = pp.tile([128, 2, CH], F32, name="z%d%d%d" % (r, c, i), tag="z", bufs=3)
                z[r, c, i] = ps
                for k in range(2):
                    t = 2 * i + k
                    nc.tensor.matmul_mx(
                        out=ps[:, k, :],
                        lhsT=wc["w%d" % r][:, 128 * t : 128 * (t + 1)].bitcast(FP8X4),
                        lhsT_scale=ws["w%d" % r][:, 128 * t : 128 * (t + 1)],
                        rhs=xc[r, c][:].bitcast(FP8X4),
                        rhs_scale=xsc[r, c][:],
                        start=True,
                        stop=True,
                    )

        def relu(r, c, eng="ssss"):
            for t in range(4):
                src = z[r, c, t // 2][:, t % 2, :].rearrange("p (j q) -> p j q", j=2)
                if eng[t] == "s":
                    nc.scalar.activation(out=u[r, c][:, :, t, :], in_=src, func=AF.Relu, bias=vec[:, r, t : t + 1])
                else:
                    nc.vector.tensor_scalar(
                        out=u[r, c][:, :, t, :], in0=src, scalar1=vec[:, r, t : t + 1], scalar2=0.0, op0=ADD, op1=MAX
                    )

        def diff(c):
            nc.vector.tensor_sub(out=dd[c][:], in0=u[0, c][:], in1=u[1, c][:])

        pst = {}
        ut = {}
        pss = {}

        def sum_t(c, plain=0):
            pst[c] = pp.tile([128, 4, 128], F32, name="pst%d" % c, tag="st", bufs=2)
            for t in range(4):
                for i in range(4):
                    nc.tensor.matmul(
                        out=pst[c][:, t, :], lhsT=u[1 - i // 2, c][:, i % 2, t, :], rhs=identf[:],
                        start=(i == 0), stop=(i == 3), is_transpose=(i >= plain),
                    )

        def sum_cp(c, eng):
            ut[c] = big("ut%d" % c, [128, 4, 128], F32)
            if eng == "v":
                nc.vector.tensor_copy(out=ut[c][:], in_=pst[c][:])
            else:
                nc.scalar.copy(out=ut[c][:], in_=pst[c][:])

        def sum_g(c):
            pss[c] = pp.tile([128, 4, CB], F32, name="pss%d" % c, tag="st", bufs=2)
            for t in range(4):
                nc.tensor.matmul(out=pss[c][:, t, :], lhsT=ut[c][:, t, :], rhs=grp[:], start=True, stop=True)

        sgb = {}
        lps = {}
        a0 = {}
        for c in range(NCH):
            sgb[c] = big("sgb%d" % c, [128, CB, 4], BF16)
            a0[c] = big("a0g%d" % c, [128, 4, CB], F32)

        def sgate(c):
            nc.vector.tensor_mul(out=sgb[c][:], in0=pss[c][:].rearrange("p t b -> p b t"), in1=gsb[:])

        def sg_q(c):
            nc.vector.quantize_mx(
                out=sgc[c][:, 0:CB].bitcast(FP8X4), scales=sgs[c][:, 0:CB], in_=sgb[c][:].rearrange("p b t -> p (b t)")
            )

        def mx2(c):
            lps[c] = pp.tile([128, 4, B], F32, name="l%d" % c, tag="l", bufs=1)
            for t in range(4):
                for i, nm in enumerate(("a0", "a1")):
                    nc.tensor.matmul_mx(
                        out=lps[c][:, t, :],
                        lhsT=wc[nm][:, 128 * t : 128 * (t + 1)].bitcast(FP8X4),
                        lhsT_scale=ws[nm][:, 128 * t : 128 * (t + 1)],
                        rhs=sgc[c][:].bitcast(FP8X4),
                        rhs_scale=sgs[c][:],
                        start=(i == 0),
                        stop=(i == 1),
                    )

        def sigm(c):
            for t in range(4):
                nc.scalar.activation(out=a0[c][:, t, :], in_=lps[c][:, t, 0:CB], func=AF.Sigmoid, bias=bd[:, t : t + 1])

        def mul_a(c, j):
            nc.vector.tensor_mul(
                out=mm[c][:, j].rearrange("p t (b i) -> p t b i", i=4),
                in0=dd[c][:, j].rearrange("p t (b i) -> p t b i", i=4),
                in1=a0[c][:].unsqueeze(3).to_broadcast([128, 4, CB, 4]),
            )

        def o_add(c, j):
            nc.vector.tensor_add(out=oo[c][:, j], in0=mm[c][:, j], in1=u[1, c][:, j])

        def obf(c, eng):
            dst = ob[c][:].rearrange("p (q i k) -> p q k i", i=2, k=8)
            src = oo[c][:].rearrange("p j t q -> p (j t) q").rearrange("p k (q i) -> p q k i", i=2)
            if eng == "v":
                nc.vector.tensor_copy(out=dst, in_=src)
            else:
                nc.scalar.copy(out=dst, in_=src)

        def o_q(c):
            nc.vector.quantize_mx(out=oc[c][:].bitcast(FP8X4), scales=osc[:, CH * c : CH * (c + 1)], in_=ob[c][:])

        ops = {}

        def o_tr(c, j, tag="tp"):
            ps = pp.tile([128, 4, 128], F32, name="o%d%d" % (c, j), tag=tag, bufs=3 if tag == "z" else 2)
            ops[c, j] = ps
            for t in range(4):
                nc.tensor.transpose(ps[:, t, :], oo[c][:, j, t, :], identf[:])

        def o_cp(c, j, eng):
            src = ops[c, j][:].rearrange("q t p -> q p t")
            if eng == "v":
                nc.vector.tensor_copy(out=ot[c][:, j], in_=src)
            else:
                nc.scalar.copy(out=ot[c][:, j], in_=src)

        rows = out_0.rearrange("b n e -> (b n) e").rearrange("(c q j) e -> c q j e", c=NCH, j=2)
        words = out_1.rearrange("g p m t -> (g p) (m t)").bitcast(I32)
        srows = out_2.rearrange("g q m -> (g q) m").bitcast(I32)

        def o_st(c):
            nc.sync.dma_start(
                out=rows[c].rearrange("q j e -> q (j e)"), in_=ot[c][:].rearrange("q j p t -> q (j p t)")
            )

        def o_st1(c, j):
            nc.sync.dma_start(out=rows[c, :, j, :], in_=ot[c][:, j].rearrange("q p t -> q (p t)"))

        def w_st(c):
            nc.sync.dma_start(out=words[:, CH * c : CH * (c + 1)], in_=oc[c][:].bitcast(I32))

        def s_st(c0, c1):
            for q in range(4):
                nc.scalar.dma_start(
                    out=srows[4 * q : 4 * q + 4, CH // 4 * c0 : CH // 4 * c1],
                    in_=osc[32 * q : 32 * q + 4, CH * c0 : CH * c1].bitcast(I32),
                )

        load_x(1, 0)
        x_tr(1, 0)
        load_x(0, 0)
        x_cp(1, 0, "s")
        load_x(0, 3)
        x_tr(0, 0)
        x_tr(0, 3)
        load_w("w1")
        x_q(1, 0)
        load_w("w0")
        load_x(1, 1)
        consts_pe()
        w_cp("w1", 2, 4, "s")
        load_x(1, 2)
        load_x(0, 1)
        x_cp(0, 0, "s")
        load_x(1, 3)
        w_cp("w0", 0, 2, "s")
        w_cp("w1", 0, 2, "v")
        w_q("w1", 0, 2)
        x_cp(0, 3, "v")
        w_q("w1", 2, 4)
        mx1(1, 0)
        x_tr(1, 1)
        x_tr(1, 2)
        consts()
        x_q(0, 0)
        w_cp("w0", 2, 4, "v")
        w_q("w0", 0, 2)
        w_q("w0", 2, 4)
        relu(1, 0, "sssv")
        x_cp(1, 1, "s")
        mx1(0, 0)
        load_w("a0")
        x_q(0, 3)
        x_q(1, 1)
        x_tr(0, 1)
        relu(0, 0, "ssss")
        x_cp(0, 1, "s")
        x_cp(1, 2, "v")
        w_cp("a0", 0, 4, "v")
        load_x(0, 2)
        diff(0)
        mx1(1, 1)
        x_q(0, 1)
        sum_t(0, 0)
        relu(1, 1, "ssss")
        x_tr(0, 2)
        x_q(1, 2)
        load_w("a1")
        w_cp("a1", 0, 4, "v")
        x_tr(1, 3)
        w_q("a0", 0, 4)
        sum_cp(0, "s")
        consts2()
        x_cp(0, 2, "s")
        w_q("a1", 0, 4)
        mx1(0, 1)
        relu(0, 1, "ssss")
        x_cp(1, 3, "s")
        x_q(0, 2)
        sum_g(0)
        mx1(1, 2)
        sgate(0)
        relu(1, 2, "ssss")
        sum_t(1, 0)
        x_q(1, 3)
        sg_q(0)
        mx1(0, 2)
        sum_cp(1, "v")
        relu(0, 2, "ssss")
        mx2(0)
        sigm(0)
        diff(1)
        sum_g(1)
        sgate(1)
        mx1(1, 3)
        diff(2)
        sum_t(2, 0)
        sg_q(1)
        mx2(1)
        relu(1, 3, "ssss")
        mul_a(0, 0)
        sum_cp(2, "s")
        mx1(0, 3)
        mul_a(0, 1)
        sigm(1)
        o_add(0, 0)
        relu(0, 3, "ssss")
        sum_g(2)
        o_add(0, 1)
        mul_a(1, 1)
        sum_t(3, 0)
        sgate(2)
        mul_a(1, 0)
        obf(0, "s")
        sg_q(2)
        sum_cp(3, "s")
        o_tr(0, 1)
        o_tr(0, 0)
        o_cp(0, 1, "s")
        diff(3)
        o_add(1, 1)
        mx2(2)
        sigm(2)
        o_cp(0, 0, "s")
        sum_g(3)
        o_add(1, 0)
        mul_a(2, 0)
        o_st(0)
        sgate(3)
        obf(1, "s")
        o_q(0)
        o_tr(1, 0)
        o_tr(1, 1)
        o_cp(1, 0, "s")
        sg_q(3)
        mx2(3)
        mul_a(2, 1)
        o_cp(1, 1, "s")
        o_st(1)
        o_add(2, 0)
        w_st(0)
        o_add(2, 1)
        sigm(3)
        obf(2, "s")
        o_q(1)
        w_st(1)
        mul_a(3, 0)
        mul_a(3, 1)
        o_add(3, 0)
        o_tr(2, 0)
        o_cp(2, 0, "s")
        o_q(2)
        o_add(3, 1)
        o_tr(2, 1)
        o_cp(2, 1, "s")
        w_st(2)
        obf(3, "v")
        o_st(2)
        o_tr(3, 0)
        o_cp(3, 0, "s")
        o_st1(3, 0)
        o_q(3)
        w_st(3)
        o_tr(3, 1)
        o_cp(3, 1, "s")
        s_st(0, 4)
        o_st1(3, 1)
